import numpy as np, ml_dtypes
CORES = [113,118,241,246]
N = 4
BF = ml_dtypes.bfloat16
def gentries(a):
    return np.ascontiguousarray(a.reshape(8, 16, -1).transpose(0, 2, 1)).reshape(8, -1)
def gtable(e):
    e = np.asarray(e); return np.ascontiguousarray(e.reshape(8, -1, 16).transpose(0, 2, 1)).reshape(128, -1).astype(np.int32)
V, CAP, D, R = 48, 16, 4, 2
def cube():
    P = np.indices((4, 4, 4, 4)).reshape(4, -1).T; P = P[(np.sort(P, 1) == np.arange(4)).all(1)]
    w = np.array([64, 16, 4, 1]); at = np.zeros(256, np.int64); at[P @ w] = np.arange(24)
    return at[P[:, P] @ w]
def cyclic():
    i = np.arange(24); return (i[:, None] + i) % 24
def dihedral():
    i = np.arange(24); r = i % 12; s = i // 12
    return (r[:, None] + np.where(s[:, None] == 1, -r, r)) % 12 + 12 * (s[:, None] ^ s)
def labelled(rng, plain=0, mixed=False):
    res = np.zeros((8, 24, 24), np.int64)
    for g in range(8):
        c = cyclic() if mixed and g in (2, 3) else dihedral() if mixed and g in (4, 5) else cube()
        lab = np.arange(24) if g < plain else rng.permutation(24)
        res[g][lab[:, None], lab[None, :]] = lab[c]
    return res
def values(rng):
    return rng.standard_normal((N, 128, V * 24), dtype=np.float32) * np.exp2(rng.integers(-2, 3, (N, 128, 1))).astype(np.float32)
def raw(rng, plain=0, mixed=False):
    q = (np.arange(N)[:, None, None, None] + 1 + rng.integers(0, N - 1, (N, 8, D, V))) % N
    slot = V + q * CAP + rng.integers(0, CAP, (N, 8, D, V)); own = rng.integers(0, V, (N, 8, D, V))
    return {"x": values(rng), "pose": rng.integers(0, 24, (N, 8, V)), "act": rng.integers(0, 24, (N, 8, R - 1, V)), "c": labelled(rng, plain, mixed),
            "shown": np.argsort(rng.random((N, 8, N, V)), -1)[..., :CAP], "nbr": np.where(rng.random((N, 8, D, V)) < 0.5, own, slot)}
def glists(a):
    return np.stack([gtable(v.reshape(8, -1)) for v in a])
def pack(d):
    c = d["c"]; rel = np.argsort(c, 2).transpose(0, 2, 1)
    every = lambda t: np.repeat(np.ascontiguousarray(t).reshape(1, 8, 576).astype(np.int32), N, 0)
    return {"x": np.ascontiguousarray(d["x"].astype(np.float32)), "pose": glists(d["pose"]), "act": glists(d["act"]), "rel": every(rel), "ct": every(c), "shown": glists(d["shown"]), "nbr": glists(d["nbr"])}
def setup_inputs(rng):
    return pack(raw(rng))
def setup_inputs_full(rng):
    d = raw(rng, mixed=True)
    for r in range(N):
        s = np.concatenate([V + q * CAP + np.arange(CAP) for q in range(N) if q != r])
        for g in range(8):
            flat = d["nbr"][r, g].reshape(-1).copy(); flat[rng.permutation(D * V)[:len(s)]] = s; d["nbr"][r, g] = flat.reshape(D, V)
    return pack(d)
def setup_inputs_repeat(rng):
    d = raw(rng); a, b, e, w = rng.permutation(N)[:4]; n = d["nbr"]
    n[a] = rng.integers(0, V, (8, D, V)); n[a, :, 0] = np.arange(V)
    n[b] = V + a * CAP + rng.integers(0, CAP, (8, D, V))
    n[e] = n[e][:, :1]; q0 = 1 if e == 0 else 0; q1 = N - 2 if e == N - 1 else N - 1
    n[e, :, :, 0] = 0; n[e, :, :, V - 1] = V - 1; n[e, :, :, 1] = V + q1 * CAP + CAP - 1; n[e, :, :, 2] = V + q0 * CAP
    d["shown"][w] = d["shown"][w][..., :1]
    return pack(d)
def setup_inputs_below(rng):
    d = raw(rng); k = rng.integers(0, 87, 8); k[rng.integers(0, 8)] = 86
    d["x"] = -rng.integers(1, 200, (N, 128, V * 24)).astype(np.float32) * np.repeat(np.exp2(k), 16)[:, None].astype(np.float32); return pack(d)
def setup_inputs_alike(rng):
    d = raw(rng, 2, True)
    for g in range(8):
        if g % 2 == 0:
            d["pose"][:, g] = rng.integers(0, 24); d["act"][:, g] = rng.integers(0, 24, (1, R - 1, 1))
        else:
            d["act"][:, g] = np.argmax((d["c"][g] == np.arange(24)).all(1))
    return pack(d)
def setup_inputs_spread(rng):
    d = raw(rng); k = (N, 1, V * 24)
    d["x"] = d["x"] * (np.exp2(rng.integers(-6, 7, k)) * (rng.random(k) > 0.0625)).astype(np.float32); return pack(d)
def check_inputs(d):
    bad = []; j = np.arange(24)
    def within(a, top): return bool((a >= 0).all() and (a < top).all())
    if not np.isfinite(d["x"]).all(): bad.append("finite")
    elif not (np.abs(d["x"]) <= 2.0 ** 94).all(): bad.append("size")
    if not within(d["pose"], 24): bad.append("pose")
    if not within(d["act"], 24): bad.append("act")
    if not within(d["shown"], V): bad.append("shown")
    for r in range(N):
        n = d["nbr"][r]
        if not within(n, V + N * CAP) or ((n >= V + r * CAP) & (n < V + r * CAP + CAP)).any(): bad.append("nbr"); break
    if not (d["rel"] == d["rel"][:1]).all() or not (d["ct"] == d["ct"][:1]).all(): bad.append("tables_alike")
    if not within(d["rel"], 24) or not within(d["ct"], 24): bad.append("tables_range")
    else:
        for g in range(8):
            c = d["ct"][0, g].reshape(24, 24).astype(np.int64); l = d["rel"][0, g].reshape(24, 24).astype(np.int64)
            if not ((np.sort(c, 1) == j).all() and (np.sort(c, 0) == j[:, None]).all() and (c[c] == c[:, c]).all()): bad.append("ct_group"); break
            if not (c[j[None, :], l] == j[:, None]).all(): bad.append("rel"); break
    return bad
def reference(x, pose, act, rel, ct, shown, nbr):
    f = x.reshape(N, 8, 16, V, 24)
    p = np.stack([gentries(v) for v in pose]).astype(np.int64)
    ac = np.stack([gentries(v) for v in act]).reshape(N, 8, R - 1, V).astype(np.int64)
    sh = np.stack([gentries(v) for v in shown]).reshape(N, 8, N, CAP)
    nb = np.stack([gentries(v) for v in nbr]).reshape(N, 8, D, V)
    for t in range(R):
        new = np.zeros(f.shape, np.float32); turned = np.zeros(p.shape, np.int64)
        for r in range(N):
            for g in range(8):
                fe = np.concatenate([f[r, g]] + [f[q, g][:, sh[q, g, r]] for q in range(N)], 1)
                pe = np.concatenate([p[r, g]] + [p[q, g][sh[q, g, r]] for q in range(N)])
                j = nb[r, g]
                e = rel[r, g][p[r, g][None, :] * 24 + pe[j]].astype(np.int64)
                k = ct[r, g][e[:, :, None] * 24 + np.arange(24)]
                new[r, g] = np.maximum.reduce(fe[:, j[:, :, None], k], axis=1)
                if t < R - 1: turned[r, g] = ct[r, g][p[r, g] * 24 + ac[r, g, t]]
        f = new; p = turned
    return {"y": np.ascontiguousarray(f.reshape(N, 128, V * 24))}

@@ -1,0 +1,320 @@
+from concourse.bass import DstId, RemoteDMATransfer
+from concourse.mybir import AluOpType, AxisListType, ActivationFunctionType
+
+NX = 110
+SCRATCH = {
+    "X": ("sbuf", [128, 1152], "float32"), "TR": ("sbuf", [128, 48], "int32"), "PO": ("sbuf", [128, 4], "int32"),
+    "SHN": ("sbuf", [128, 4], "int32"), "NB": ("sbuf", [128, 12], "int32"), "AC": ("sbuf", [128, 4], "int32"),
+    "R8": ("sbuf", [8, 576], "int32"),
+    "IP": ("sbuf", [128, 2], "int32"), "DD": ("sbuf", [128, 128], "float32"), "IM": ("sbuf", [128, 48], "int32"),
+    "IM2": ("sbuf", [128, 48], "int32"), "BO": ("sbuf", [8, 128], "int32"), "BO2": ("sbuf", [8, 128], "int32"),
+    "CI": ("sbuf", [128, 192], "float32"), "C48": ("sbuf", [128, 96], "float32"), "T16": ("sbuf", [128, 16], "float32"),
+    "N4": ("sbuf", [128, 4], "float32"), "AT": ("sbuf", [128, 112], "float32"),
+    "B1": ("sbuf", [128, 2], "int32"), "B8": ("sbuf", [128, 2], "int32"), "LO": ("sbuf", [128, 1], "float32"),
+    "HI": ("sbuf", [128, 1], "float32"), "P48": ("sbuf", [128, 1], "float32"), "P192": ("sbuf", [128, 1], "float32"),
+    "P24": ("sbuf", [128, 4], "float32"), "SH": ("sbuf", [128, 128], "bfloat16"), "SL": ("sbuf", [128, 128], "bfloat16"),
+    "MK": ("sbuf", [128, 48], "float32"), "BN": ("sbuf", [8, 128], "bfloat16"), "NP": ("sbuf", [128, 4], "float32"),
+    "TRB": ("sbuf", [128, 48], "bfloat16"), "WT": ("sbuf", [128, 96], "float32"), "LP": ("sbuf", [128, 12], "uint16"),
+    "NN": ("sbuf", [128, 192], "float32"), "LSH": ("sbuf", [128, 4], "uint16"), "SHF": ("sbuf", [128, 4], "float32"),
+    "R1": ("sbuf", [128, 48], "float32"), "R2": ("sbuf", [128, 48], "float32"), "K1": ("sbuf", [128, 24], "float32"),
+    "LA": ("sbuf", [128, 72], "uint16"), "KO": ("sbuf", [128, 24], "float32"), "OWN": ("sbuf", [128, 72], "uint16"),
+    "R8B": ("sbuf", [8, 576], "bfloat16"), "REL": ("sbuf", [128, 576], "float32"), "NBU": ("sbuf", [128, 12], "uint16"),
+    "ACF": ("sbuf", [128, 4], "float32"), "ID24": ("sbuf", [128, 1], "float32"),
+    "L1": ("sbuf", [128, 4], "uint16"), "L2": ("sbuf", [128, 4], "uint16"), "L3": ("sbuf", [128, 4], "uint16"),
+    "M1": ("sbuf", [128, 48], "float32"), "M2": ("sbuf", [128, 48], "float32"), "M3": ("sbuf", [128, 48], "float32"),
+    "WV": ("sbuf", [128, 4], "float32"), "VV": ("sbuf", [128, 4], "float32"), "EV": ("sbuf", [128, 4], "float32"),
+    "LE": ("sbuf", [128, 48], "uint16"), "ARM": ("sbuf", [128, 768], "float32"), "ARX": ("sbuf", [128, 192], "float32"),
+    "ZZ": ("sbuf", [128, 768], "float32"), "LSZ": ("sbuf", [128, 12], "uint16"),
+    "ZS1": ("sbuf", [128, 192], "float32"), "ZS2": ("sbuf", [128, 192], "float32"), "KB": ("sbuf", [128, 96], "float32"),
+    "LB": ("sbuf", [128, 288], "uint16"), "KC": ("sbuf", [128, 96], "float32"), "LC": ("sbuf", [128, 288], "uint16"),
+    "LEY": ("sbuf", [128, 12], "uint16"), "ZY1": ("sbuf", [128, 192], "float32"), "ZY2": ("sbuf", [128, 192], "float32"),
+    "KY": ("sbuf", [128, 96], "float32"), "LY": ("sbuf", [128, 288], "uint16"),
+    "W0": ("sbuf", [128, 2304], "float32"), "W1": ("sbuf", [128, 2304], "float32"),
+    "SA": ("sbuf", [128, 1152], "float32"), "SB": ("sbuf", [128, 1152], "float32"), "YB": ("sbuf", [128, 1152], "float32"),
+    "G2": ("sbuf", [128, 3456], "float32"), "G3": ("sbuf", [128, 3456], "float32"),
+    "H1": ("sbuf", [128, 3456], "float32"), "H2": ("sbuf", [128, 3456], "float32"), "H0": ("sbuf", [128, 1024], "float32"),
+    "PT": ("psum", [128, 512], "float32"), "PR": ("psum", [128, 1024], "float32"),
+    "PC0": ("psum", [128, 512], "float32"), "PC1": ("psum", [128, 512], "float32"), "PC2": ("psum", [128, 512], "float32"),
+}
+SEMAPHORES = (["self_v", "self_s", "self_t", "self_g", "self_y", "left"] + ["arr%d_%d" % (t, q) for t in range(2) for q in range(4)]
+              + ["x%d" % k for k in range(NX)])
+OWNW, SLW = 48 * 24, 16 * 24
+
+
+def place(q, p):
+    return OWNW + SLW * (q if q < p else q - 1)
+
+
+def rank_program(g, core, T, topo):
+    r = T.rank_of(core)
+    if r is None:
+        return
+    A, ACT = AluOpType, ActivationFunctionType
+    ops = []
+
+    def op(q, f, deps=(), kind="c"):
+        ops.append({"q": q, "f": f, "deps": list(deps), "kind": kind})
+        return len(ops) - 1
+
+    v, s, t = g.vector, g.scalar, g.tensor
+    queues = {"v": v, "s": s, "t": t, "g": g, "y": g.sync}
+
+    def ts(out, in0, s1, op0, s2=None, op1=None, deps=()):
+        if op1 is None:
+            return op("v", lambda: v.tensor_scalar(out, in0, s1, None, op0), deps)
+        return op("v", lambda: v.tensor_scalar(out, in0, s1, s2, op0, op1), deps)
+
+    def tt(out, a, b, o, deps=()):
+        return op("v", lambda: v.tensor_tensor(out, a, b, o), deps)
+
+    def cp(out, a, deps=()):
+        return op("v", lambda: v.tensor_copy(out, a), deps)
+
+    def ac(out, a, deps=(), scale=None):
+        if scale is None:
+            return op("s", lambda: s.activation(out, a, ACT.Copy), deps)
+        return op("s", lambda: s.activation(out, a, ACT.Identity, scale=scale), deps)
+
+    def ld(q, out, in_, deps=()):
+        return op(q, lambda: queues[q].dma_start(out, in_), deps, "d")
+
+    others = [p for p in range(len(T.cores)) if p != r]
+    near = [p for p in others if T.cores[p] in topo.cores_of(core)]
+    far = [p for p in others if p not in near]
+    far.sort(key=lambda p: topo.die(T.cores[p]) != topo.die(core))
+    dest = far + near
+    feng = topo.engines(core, T.cores[far[0]])
+    neng = [e for e in topo.engines(core, T.cores[near[0]]) if e not in feng]
+
+    def bits(es):
+        return sum(1 << e for e in es)
+
+    d_ra = ld("y", T.TR[:, 0:24], T.rel[:, 0:384])
+    d_po = ld("s", T.PO[:, 0:3], T.pose[:, :])
+    d_rd = ld("y", T.TR[:, 24:48], T.rel[:, 192:576])
+    d_sh = ld("s", T.SHN[:, 0:4], T.shown[:, :])
+    d_x = ld("s", T.X[:, :], T.x[:, :])
+    d_nb = ld("y", T.NB[:, 0:12], T.nbr[:, :])
+    d_r8 = ld("y", T.R8[:, :], T.rel[:, :])
+    d_ac = ld("y", T.AC[:, 0:3], T.act[:, :])
+
+    def iota(out, pat, base, cm, f32=True):
+        if f32:
+            return op("g", lambda: g.iota(out, pat, base, cm, allow_small_or_imprecise_dtypes=True))
+        return op("g", lambda: g.iota(out, pat, base, cm))
+
+    i_p = iota(T.IP[:, :], [[0, 2]], 0, 1, False)
+    i_d = iota(T.DD[:, :], [[1, 128]], 0, -1)
+    i_c = iota(T.C48[:, :], [[0, 2], [24, 48]], 0, 0)
+    i_b = iota(T.BO[:, :], [[1, 128]], 0, -16, False)
+    i_m = iota(T.IM[:, :], [[0, 3], [1, 16]], 0, -1, False)
+    hole = 48 + 16 * r + 16
+    i_a = [iota(T.AT[:, 0:hole], [[24, hole]], 0, 0)]
+    if hole < 112:
+        i_a.append(iota(T.AT[:, hole:112], [[24, 112 - hole]], 24 * (hole - 16), 0))
+    i_t = iota(T.T16[:, :], [[24, 4], [0, 4]], 0, 0)
+    i_n = iota(T.N4[:, :], [[48, 4]], 0, 0)
+
+    c_1 = ts(T.B1[:, :], T.IP[:, :], 1, A.bitwise_and, deps=[i_p])
+    c_8 = ts(T.B8[:, :], T.IP[:, :], 8, A.bitwise_and, deps=[i_p])
+    c_lo = ts(T.LO[:, :], T.B8[:, 0:1], 0, A.is_equal, deps=[c_1, c_8])
+    c_hi = ts(T.HI[:, :], T.B8[:, 0:1], 0, A.is_gt, deps=[c_8])
+    c_48 = ts(T.P48[:, :], T.B1[:, 0:1], 48, A.mult, deps=[c_1])
+    c_192 = ts(T.P192[:, :], T.B1[:, 0:1], 192, A.mult, deps=[c_1])
+    c_sh = ts(T.SH[:, :], T.DD[:, :], -8, A.is_equal, T.HI[:, :], A.mult, deps=[i_d, c_hi])
+    c_sl = ts(T.SL[:, :], T.DD[:, :], 8, A.is_equal, T.LO[:, :], A.mult, deps=[i_d, c_lo])
+    c_ci = [cp(T.CI[:, 0:96], T.C48[:, :], deps=[i_c]),
+            ts(T.CI[:, 96:144], T.C48[:, 0:48], T.LO[:, :], A.mult, deps=[i_c, c_lo]),
+            ts(T.CI[:, 144:192], T.C48[:, 0:48], T.HI[:, :], A.mult, deps=[i_c, c_hi])]
+
+    lp = [ts(T.LP[:, 3 * k:3 * k + 3], T.PO[:, 0:3], 24 * k, A.add, deps=[d_po]) for k in range(4)]
+    lsh = [ts(T.LSH[:, k:k + 1], T.SHN[:, p:p + 1], T.P48[:, :], A.add, deps=[d_sh, c_48]) for k, p in enumerate(dest)]
+    trb = cp(T.TRB[:, :], T.TR[:, :], deps=[d_ra, d_rd])
+    wt1 = cp(T.WT[:, 0:48], T.TR[:, :], deps=[d_ra, d_rd])
+    m1 = op("t", lambda: t.matmul(T.PT[:, 0:24], T.SH[:, :], T.TRB[:, 24:48], True, True), [trb, c_sh])
+    m2 = op("t", lambda: t.matmul(T.PT[:, 24:48], T.SL[:, :], T.TRB[:, 0:24], True, True), [trb, c_sl])
+    wt2 = cp(T.WT[:, 48:96], T.PT[:, 0:48], deps=[m1, m2])
+    nn = tt(T.NN[:, :], T.WT[:, :].indirect(T.LP[:, 0:12]), T.CI[:, :], A.add, deps=lp + [wt1, wt2] + c_ci)
+    r1 = cp(T.R1[:, :], T.NN[:, 0:96].indirect(T.LSH[:, 0:3]), deps=[nn] + lsh)
+    r2 = cp(T.R2[:, :], T.NN[:, 96:192].indirect(T.LSH[:, 0:3]), deps=[nn] + lsh)
+    la = [cp(T.LA[:, 0::3], T.R1[:, 0::2], deps=[r1]), cp(T.LA[:, 2::3], T.R1[:, 1::2], deps=[r1])]
+    k1 = tt(T.K1[:, :], T.R2[:, 0::2], T.R2[:, 1::2], A.add, deps=[r2])
+    la.append(cp(T.LA[:, 1::3], T.K1[:, :], deps=[k1]))
+
+    sa = []
+    for k in range(3):
+        a, b = SLW * k, SLW * k + SLW // 2
+        sa.append([cp(T.SA[:, a:b], T.X[:, :].indirect(T.LA[:, 24 * k:24 * k + 12]), deps=la + [d_x]),
+                   ac(T.SA[:, b:a + SLW], T.X[:, :].indirect(T.LA[:, 24 * k + 12:24 * k + 24]), deps=la + [d_x])])
+
+    def addr(p):
+        return topo.addr(T.cores[p], core)
+
+    def transfer(p, buf, win, k, es, arr):
+        rid, pid = addr(p)
+        c = place(r, p)
+        return RemoteDMATransfer(src=buf[:, SLW * k:SLW * k + SLW], dst=win[:, c:c + SLW], dst_ids=[DstId(rid=rid, pnc=pid)],
+                                 dma_engine_mask=bits(es), remote_sem=T.sem[arr])
+
+    def send(p, buf, win, k, es, arr, deps):
+        rid, pid = addr(p)
+        c = place(r, p)
+        return op("g", lambda: g.remote_dma(win[:, c:c + SLW], buf[:, SLW * k:SLW * k + SLW], T.sem[arr], T.sem["left"], pid, rid,
+                                            bits(es)), deps, "r")
+
+    left = [0]
+    half = [feng[:len(feng) // 2], feng[len(feng) // 2:]]
+    got0 = {}
+    op("g", lambda: g.remote_dma_fused([transfer(p, T.SA, T.W0, k, half[k], "arr0_%d" % r) for k, p in enumerate(far)],
+                                       local_sem=T.sem["left"]), sa[0] + sa[1], "r")
+    send(near[0], T.SA, T.W0, 2, neng, "arr0_%d" % r, sa[2])
+    left[0] += len(feng) + len(neng)
+    arr0 = [("sem", "arr0_%d" % q, len(half[0]) if q in far else len(neng)) for q in others]
+
+    r8b = cp(T.R8B[:, :], T.R8[:, :], deps=[d_r8])
+    b2 = ts(T.BO2[:, :], T.BO[:, :], 4, A.arith_shift_right, deps=[i_b])
+    bn = ts(T.BN[:, :], T.BO2[:, :], 0, A.is_equal, deps=[b2])
+    pr = [op("t", lambda: t.matmul(T.PR[:, 0:288], T.BN[:, :], T.R8B[:, 0:288], True, True), [bn, r8b]),
+          op("t", lambda: t.matmul(T.PR[:, 512:800], T.BN[:, :], T.R8B[:, 288:576], True, True), [bn, r8b])]
+    nbu = cp(T.NBU[:, :], T.NB[:, :], deps=[d_nb])
+    rel = [ac(T.REL[:, 0:288], T.PR[:, 0:288], deps=[pr[0]]), ac(T.REL[:, 288:576], T.PR[:, 512:800], deps=[pr[1]])]
+    ow = [cp(T.OWN[:, 0::3], T.NN[:, 0:48:2], deps=[nn]), cp(T.OWN[:, 2::3], T.NN[:, 49:96:2], deps=[nn])]
+    ko = tt(T.KO[:, :], T.NN[:, 96:144:2], T.NN[:, 145:192:2], A.add, deps=[nn])
+    acf = cp(T.ACF[:, 0:3], T.AC[:, 0:3], deps=[d_ac])
+    ow.append(cp(T.OWN[:, 1::3], T.KO[:, :], deps=[ko]))
+    im2 = ts(T.IM2[:, :], T.IM[:, :], 15, A.bitwise_and, deps=[i_m])
+    npc = ts(T.NP[:, :], T.N4[:, :], T.P192[:, :], A.add, deps=[i_n, c_192])
+    p24 = ts(T.P24[:, :], T.N4[:, :], 0, A.mult, T.P48[:, :], A.add, deps=[i_n, c_48])
+    mk = ts(T.MK[:, :], T.IM2[:, :], 0, A.is_equal, deps=[im2])
+    shf = cp(T.SHF[:, :], T.SHN[:, :], deps=[d_sh])
+    p24 = ts(T.P24[:, :], T.P24[:, :], 0.5, A.mult, deps=[p24])
+    lsz = [ts(T.LSZ[:, 4 * k:4 * k + 4], T.NP[:, :], T.SHF[:, p:p + 1], A.add, deps=[npc, shf]) for k, p in enumerate(dest)]
+    arm = [ac(T.ARM[:, 192 * k:192 * k + 192], T.AT[:, :].indirect(T.NBU[:, :]), deps=i_a + [nbu] + [c_lo, c_hi],
+              scale=[None, None, T.LO[:, :], T.HI[:, :]][k]) for k in range(4)]
+    own0 = ac(T.W0[:, 0:OWNW], T.X[:, :].indirect(T.OWN[:, :]), deps=ow + [d_x])
+    arx = [ac(T.ARX[:, 0::2], T.ARM[:, 384:576:2], deps=[arm[2]]), ac(T.ARX[:, 1::2], T.ARM[:, 577:768:2], deps=[arm[3]])]
+
+    def level(lst, ldeps, tmp, out):
+        m = tt(tmp[:, :], T.REL[:, :].indirect(lst[:, 0:3]), T.MK[:, :], A.mult, deps=rel + [mk] + ldeps)
+        return [op("v", lambda c=c: v.tensor_reduce(out[:, c:c + 1], tmp[:, 16 * c:16 * c + 16], AxisListType.X, A.add), [m])
+                for c in range(3)]
+
+    idc = ts(T.ID24[:, :], T.REL[:, 0:1], 24, A.mult, deps=[rel[0]])
+    l1 = ts(T.L1[:, 0:3], T.PO[:, 0:3], T.ID24[:, :], A.add, deps=[idc, d_po])
+    wv = level(T.L1, [l1], T.M1, T.WV)
+    l2 = [ts(T.L2[:, c:c + 1], T.WV[:, c:c + 1], 24, A.mult, T.ACF[:, c:c + 1], A.add, deps=wv + [acf]) for c in range(3)]
+    vv = level(T.L2, l2, T.M2, T.VV)
+    l3 = [ts(T.L3[:, c:c + 1], T.WV[:, c:c + 1], 24, A.mult, T.VV[:, c:c + 1], A.add, deps=wv + vv) for c in range(3)]
+    ev = level(T.L3, l3, T.M3, T.EV)
+    le = [ts(T.LE[:, c::3], T.T16[:, :], T.EV[:, c:c + 1], A.add, deps=[i_t] + ev) for c in range(3)]
+    zz = tt(T.ZZ[:, :], T.WT[:, :].indirect(T.LE[:, :]), T.ARM[:, :], A.add, deps=le + arm)
+    zs1 = cp(T.ZS1[:, :], T.ZZ[:, 0:384].indirect(T.LSZ[:, :]), deps=[zz] + lsz)
+    zs2 = cp(T.ZS2[:, :], T.ZZ[:, 384:768].indirect(T.LSZ[:, :]), deps=[zz] + lsz)
+    lb = [cp(T.LB[:, 0::3], T.ZS1[:, 0::2], deps=[zs1]), cp(T.LB[:, 2::3], T.ZS1[:, 1::2], deps=[zs1])]
+    kb = tt(T.KB[:, :], T.ZS2[:, 0::2], T.ZS2[:, 1::2], A.add, deps=[zs2])
+    kc = tt(T.KC[:, :], T.ZZ[:, 384:576:2], T.ZZ[:, 577:768:2], A.add, deps=[zz])
+    lb.append(cp(T.LB[:, 1::3], T.KB[:, :], deps=[kb]))
+    lc = [cp(T.LC[:, 0::3], T.ZZ[:, 0:192:2], deps=[zz]), cp(T.LC[:, 2::3], T.ZZ[:, 193:384:2], deps=[zz]),
+          cp(T.LC[:, 1::3], T.KC[:, :], deps=[kc])]
+
+    pc = [T.PC0, T.PC1, T.PC2]
+    last_merge = [None, None, None]
+    nch, spare = [0], [0]
+
+    def piece(win, lists, width, out, deps, first):
+        b = nch[0] % 3
+        nch[0] += 1
+        c = spare[0]
+        spare[0] += width
+        P = pc[b][:, 0:width]
+        G2, G3, H1, H2 = [T[x][:, c:c + width] for x in ("G2", "G3", "H1", "H2")]
+        src = [win[:, :].indirect(x) for x in lists]
+        free = [last_merge[b]] if last_merge[b] is not None else []
+        if first:
+            H0 = T.H0[:, first - 512:first - 512 + width]
+            g3 = ac(G3, src[3], deps)
+            p3 = ac(P, G3, [g3] + free)
+            h0 = cp(H0, src[0], deps)
+            h1 = tt(H1, src[1], H0, A.max, deps + [h0])
+            h2 = tt(H2, src[2], H1, A.max, deps + [h1])
+        else:
+            g2 = ac(G2, src[2], deps)
+            g3 = ac(G3, src[3], deps)
+            p3 = ac(P, G3, [g3] + free)
+            h1 = tt(H1, src[0], G2, A.max, deps + [g2])
+            h2 = tt(H2, src[1], H1, A.max, deps + [h1])
+        res = tt(out, H2, P, A.max, [h2, p3])
+        last_merge[b] = res
+        return res
+
+    for k, p in enumerate(dest):
+        x = piece(T.W0, [T.LB[:, 96 * k + 24 * n:96 * k + 24 * n + 24] for n in range(4)], SLW, T.SB[:, SLW * k:SLW * k + SLW],
+                  lb + [own0] + arr0, 512 if k == 0 else 0)
+        es = feng if p in far else neng
+        send(p, T.SB, T.W1, k, es, "arr1_%d" % r, [x])
+        left[0] += len(es)
+    arr1 = [("sem", "arr1_%d" % q, len(feng) if q in far else len(neng)) for q in others]
+    own1 = []
+    for k in range(3):
+        own1.append(piece(T.W0, [T.LC[:, 72 * n + 24 * k:72 * n + 24 * k + 24] for n in range(4)], SLW,
+                          T.W1[:, SLW * k:SLW * k + SLW], lc + [own0] + arr0, 0))
+
+    ley = [ts(T.LEY[:, c::3], T.P24[:, :], T.VV[:, c:c + 1], A.add, deps=vv + [p24]) for c in range(3)]
+    zy1 = tt(T.ZY1[:, :], T.WT[:, 0:48].indirect(T.LEY[:, :]), T.ARM[:, 0:192], A.add, deps=ley + arm)
+    zy2 = tt(T.ZY2[:, :], T.WT[:, 48:96].indirect(T.LEY[:, :]), T.ARX[:, :], A.add, deps=ley + arx)
+    ly = [cp(T.LY[:, 0::3], T.ZY1[:, 0::2], deps=[zy1]), cp(T.LY[:, 2::3], T.ZY1[:, 1::2], deps=[zy1])]
+    ky = tt(T.KY[:, :], T.ZY2[:, 0::2], T.ZY2[:, 1::2], A.add, deps=[zy2])
+    ly.append(cp(T.LY[:, 1::3], T.KY[:, :], deps=[ky]))
+
+    stores, a = [], 0
+    for k, nodes in enumerate((16, 20, 12)):
+        c0, cw = a // 2 * 3, nodes // 2 * 3
+        x = piece(T.W1, [T.LY[:, 72 * n + c0:72 * n + c0 + cw] for n in range(4)], nodes * 24,
+                  T.YB[:, a * 24:(a + nodes) * 24], ly + own1 + arr1, 1024 if k == 0 else 0)
+        stores.append(ld("y", T.y[:, a * 24:(a + nodes) * 24], T.YB[:, a * 24:(a + nodes) * 24], [x]))
+        a += nodes
+    op("y", None, stores, "w")
+    op("g", None, [("sem", "left", left[0])], "w")
+
+    users = [[] for _ in ops]
+    for o in ops:
+        for d in o["deps"]:
+            if not isinstance(d, tuple):
+                users[d].append(o["q"])
+    names, made = {}, [0]
+    for k, o in enumerate(ops):
+        if o["kind"] in "cd" and users[k]:
+            if o["kind"] == "c" and all(q == o["q"] for q in users[k]):
+                names[k] = ("self_" + o["q"], 0)
+            else:
+                names[k] = ("x%d" % made[0], 16 if o["kind"] == "d" else 1)
+                made[0] += 1
+    done = {q: {} for q in queues}
+    count = {q: 0 for q in queues}
+
+    def wait(q, name, val):
+        if done[q].get(name, 0) < val:
+            queues[q].wait_ge(T.sem[name], val)
+            done[q][name] = val
+
+    for k, o in enumerate(ops):
+        q = o["q"]
+        for d in o["deps"]:
+            if isinstance(d, tuple):
+                wait(q, d[1], d[2])
+            elif names[d][1] == 0:
+                wait(q, names[d][0], count[q])
+            else:
+                wait(q, names[d][0], names[d][1])
+        if o["kind"] == "w":
+            continue
+        ins = o["f"]()
+        if k in names:
+            if names[k][1] == 0:
+                count[q] += 1
+                ins.then_inc(T.sem[names[k][0]], 1)
+            else:
+                ins.then_inc(T.sem[names[k][0]], names[k][1])
+    for q in queues:
+        if count[q]:
+            wait(q, "self_" + q, count[q])

@@ -5,20 +5,21 @@ NX = 110
 SCRATCH = {
     "X": ("sbuf", [128, 1152], "float32"), "TR": ("sbuf", [128, 48], "int32"), "PO": ("sbuf", [128, 4], "int32"),
     "SHN": ("sbuf", [128, 4], "int32"), "NB": ("sbuf", [128, 12], "int32"), "AC": ("sbuf", [128, 4], "int32"),
-    "R8": ("sbuf", [8, 576], "int32"),
+    "REL": ("sbuf", [128, 576], "int32"),
     "IP": ("sbuf", [128, 2], "int32"), "DD": ("sbuf", [128, 128], "float32"), "IM": ("sbuf", [128, 48], "int32"),
-    "IM2": ("sbuf", [128, 48], "int32"), "BO": ("sbuf", [8, 128], "int32"), "BO2": ("sbuf", [8, 128], "int32"),
+    "IM2": ("sbuf", [128, 48], "int32"),
     "CI": ("sbuf", [128, 192], "float32"), "C48": ("sbuf", [128, 96], "float32"), "T16": ("sbuf", [128, 16], "float32"),
     "N4": ("sbuf", [128, 4], "float32"), "AT": ("sbuf", [128, 112], "float32"),
     "B1": ("sbuf", [128, 2], "int32"), "B8": ("sbuf", [128, 2], "int32"), "LO": ("sbuf", [128, 1], "float32"),
     "HI": ("sbuf", [128, 1], "float32"), "P48": ("sbuf", [128, 1], "float32"), "P192": ("sbuf", [128, 1], "float32"),
-    "P24": ("sbuf", [128, 4], "float32"), "SH": ("sbuf", [128, 128], "bfloat16"), "SL": ("sbuf", [128, 128], "bfloat16"),
-    "MK": ("sbuf", [128, 48], "float32"), "BN": ("sbuf", [8, 128], "bfloat16"), "NP": ("sbuf", [128, 4], "float32"),
+    "P24C": ("sbuf", [128, 1], "float32"), "P24": ("sbuf", [128, 4], "float32"),
+    "SH": ("sbuf", [128, 128], "bfloat16"), "SL": ("sbuf", [128, 128], "bfloat16"),
+    "MK": ("sbuf", [128, 48], "float32"), "NP": ("sbuf", [128, 4], "float32"),
     "TRB": ("sbuf", [128, 48], "bfloat16"), "WT": ("sbuf", [128, 96], "float32"), "LP": ("sbuf", [128, 12], "uint16"),
     "NN": ("sbuf", [128, 192], "float32"), "LSH": ("sbuf", [128, 4], "uint16"), "SHF": ("sbuf", [128, 4], "float32"),
     "R1": ("sbuf", [128, 48], "float32"), "R2": ("sbuf", [128, 48], "float32"), "K1": ("sbuf", [128, 24], "float32"),
     "LA": ("sbuf", [128, 72], "uint16"), "KO": ("sbuf", [128, 24], "float32"), "OWN": ("sbuf", [128, 72], "uint16"),
-    "R8B": ("sbuf", [8, 576], "bfloat16"), "REL": ("sbuf", [128, 576], "float32"), "NBU": ("sbuf", [128, 12], "uint16"),
+    "NBU": ("sbuf", [128, 12], "uint16"),
     "ACF": ("sbuf", [128, 4], "float32"), "ID24": ("sbuf", [128, 1], "float32"),
     "L1": ("sbuf", [128, 4], "uint16"), "L2": ("sbuf", [128, 4], "uint16"), "L3": ("sbuf", [128, 4], "uint16"),
     "M1": ("sbuf", [128, 48], "float32"), "M2": ("sbuf", [128, 48], "float32"), "M3": ("sbuf", [128, 48], "float32"),
@@ -30,10 +31,12 @@ SCRATCH = {
     "LEY": ("sbuf", [128, 12], "uint16"), "ZY1": ("sbuf", [128, 192], "float32"), "ZY2": ("sbuf", [128, 192], "float32"),
     "KY": ("sbuf", [128, 96], "float32"), "LY": ("sbuf", [128, 288], "uint16"),
     "W0": ("sbuf", [128, 2304], "float32"), "W1": ("sbuf", [128, 2304], "float32"),
-    "SA": ("sbuf", [128, 1152], "float32"), "SB": ("sbuf", [128, 1152], "float32"), "YB": ("sbuf", [128, 1152], "float32"),
-    "G2": ("sbuf", [128, 3456], "float32"), "G3": ("sbuf", [128, 3456], "float32"),
-    "H1": ("sbuf", [128, 3456], "float32"), "H2": ("sbuf", [128, 3456], "float32"), "H0": ("sbuf", [128, 1024], "float32"),
-    "PT": ("psum", [128, 512], "float32"), "PR": ("psum", [128, 1024], "float32"),
+    "SA": ("sbuf", [128, 1152], "float32"), "YB": ("sbuf", [128, 1152], "float32"),
+    "F0": ("sbuf", [128, 1152], "float32"), "F1": ("sbuf", [128, 1152], "float32"),
+    "F2": ("sbuf", [128, 1152], "float32"), "F3": ("sbuf", [128, 1152], "float32"),
+    "G2": ("sbuf", [128, 2304], "float32"), "G3": ("sbuf", [128, 2304], "float32"),
+    "H0": ("sbuf", [128, 512], "float32"), "H1": ("sbuf", [128, 2304], "float32"), "H2": ("sbuf", [128, 2304], "float32"),
+    "PT": ("psum", [128, 512], "float32"),
     "PC0": ("psum", [128, 512], "float32"), "PC1": ("psum", [128, 512], "float32"), "PC2": ("psum", [128, 512], "float32"),
 }
 SEMAPHORES = (["self_v", "self_s", "self_t", "self_g", "self_y", "left"] + ["arr%d_%d" % (t, q) for t in range(2) for q in range(4)]
@@ -52,8 +55,8 @@ def rank_program(g, core, T, topo):
     A, ACT = AluOpType, ActivationFunctionType
     ops = []
 
-    def op(q, f, deps=(), kind="c"):
-        ops.append({"q": q, "f": f, "deps": list(deps), "kind": kind})
+    def op(q, f, deps=(), kind="c", grp=None):
+        ops.append({"q": q, "f": f, "deps": list(deps), "kind": kind, "grp": grp})
         return len(ops) - 1
 
     v, s, t = g.vector, g.scalar, g.tensor
@@ -75,8 +78,8 @@ def rank_program(g, core, T, topo):
             return op("s", lambda: s.activation(out, a, ACT.Copy), deps)
         return op("s", lambda: s.activation(out, a, ACT.Identity, scale=scale), deps)
 
-    def ld(q, out, in_, deps=()):
-        return op(q, lambda: queues[q].dma_start(out, in_), deps, "d")
+    def ld(q, out, in_, deps=(), grp=None):
+        return op(q, lambda: queues[q].dma_start(out, in_), deps, "d", grp)
 
     others = [p for p in range(len(T.cores)) if p != r]
     near = [p for p in others if T.cores[p] in topo.cores_of(core)]
@@ -95,8 +98,8 @@ def rank_program(g, core, T, topo):
     d_sh = ld("s", T.SHN[:, 0:4], T.shown[:, :])
     d_x = ld("s", T.X[:, :], T.x[:, :])
     d_nb = ld("y", T.NB[:, 0:12], T.nbr[:, :])
-    d_r8 = ld("y", T.R8[:, :], T.rel[:, :])
     d_ac = ld("y", T.AC[:, 0:3], T.act[:, :])
+    rel = [ld("y", T.REL[q::16, :], T.rel[:, :], [d_rd], "rel") for q in range(16)]
 
     def iota(out, pat, base, cm, f32=True):
         if f32:
@@ -106,14 +109,13 @@ def rank_program(g, core, T, topo):
     i_p = iota(T.IP[:, :], [[0, 2]], 0, 1, False)
     i_d = iota(T.DD[:, :], [[1, 128]], 0, -1)
     i_c = iota(T.C48[:, :], [[0, 2], [24, 48]], 0, 0)
-    i_b = iota(T.BO[:, :], [[1, 128]], 0, -16, False)
     i_m = iota(T.IM[:, :], [[0, 3], [1, 16]], 0, -1, False)
+    i_n = iota(T.N4[:, :], [[48, 4]], 0, 0)
+    i_t = iota(T.T16[:, :], [[24, 4], [0, 4]], 0, 0)
     hole = 48 + 16 * r + 16
     i_a = [iota(T.AT[:, 0:hole], [[24, hole]], 0, 0)]
     if hole < 112:
         i_a.append(iota(T.AT[:, hole:112], [[24, 112 - hole]], 24 * (hole - 16), 0))
-    i_t = iota(T.T16[:, :], [[24, 4], [0, 4]], 0, 0)
-    i_n = iota(T.N4[:, :], [[48, 4]], 0, 0)
 
     c_1 = ts(T.B1[:, :], T.IP[:, :], 1, A.bitwise_and, deps=[i_p])
     c_8 = ts(T.B8[:, :], T.IP[:, :], 8, A.bitwise_and, deps=[i_p])
@@ -121,22 +123,27 @@ def rank_program(g, core, T, topo):
     c_hi = ts(T.HI[:, :], T.B8[:, 0:1], 0, A.is_gt, deps=[c_8])
     c_48 = ts(T.P48[:, :], T.B1[:, 0:1], 48, A.mult, deps=[c_1])
     c_192 = ts(T.P192[:, :], T.B1[:, 0:1], 192, A.mult, deps=[c_1])
+    c_24 = ts(T.P24C[:, :], T.B1[:, 0:1], 24, A.mult, deps=[c_1])
     c_sh = ts(T.SH[:, :], T.DD[:, :], -8, A.is_equal, T.HI[:, :], A.mult, deps=[i_d, c_hi])
     c_sl = ts(T.SL[:, :], T.DD[:, :], 8, A.is_equal, T.LO[:, :], A.mult, deps=[i_d, c_lo])
     c_ci = [cp(T.CI[:, 0:96], T.C48[:, :], deps=[i_c]),
             ts(T.CI[:, 96:144], T.C48[:, 0:48], T.LO[:, :], A.mult, deps=[i_c, c_lo]),
             ts(T.CI[:, 144:192], T.C48[:, 0:48], T.HI[:, :], A.mult, deps=[i_c, c_hi])]
+    im2 = ts(T.IM2[:, :], T.IM[:, :], 15, A.bitwise_and, deps=[i_m])
+    npc = ts(T.NP[:, :], T.N4[:, :], T.P192[:, :], A.add, deps=[i_n, c_192])
+    p24 = ts(T.P24[:, :], T.N4[:, :], 0, A.mult, T.P24C[:, :], A.add, deps=[i_n, c_24])
+    mk = ts(T.MK[:, :], T.IM2[:, :], 0, A.is_equal, deps=[im2])
 
-    lp = [ts(T.LP[:, 3 * k:3 * k + 3], T.PO[:, 0:3], 24 * k, A.add, deps=[d_po]) for k in range(4)]
-    lsh = [ts(T.LSH[:, k:k + 1], T.SHN[:, p:p + 1], T.P48[:, :], A.add, deps=[d_sh, c_48]) for k, p in enumerate(dest)]
     trb = cp(T.TRB[:, :], T.TR[:, :], deps=[d_ra, d_rd])
-    wt1 = cp(T.WT[:, 0:48], T.TR[:, :], deps=[d_ra, d_rd])
     m1 = op("t", lambda: t.matmul(T.PT[:, 0:24], T.SH[:, :], T.TRB[:, 24:48], True, True), [trb, c_sh])
     m2 = op("t", lambda: t.matmul(T.PT[:, 24:48], T.SL[:, :], T.TRB[:, 0:24], True, True), [trb, c_sl])
+    wt1 = cp(T.WT[:, 0:48], T.TR[:, :], deps=[d_ra, d_rd])
+    lp = [ts(T.LP[:, 3 * k:3 * k + 3], T.PO[:, 0:3], 24 * k, A.add, deps=[d_po]) for k in range(4)]
     wt2 = cp(T.WT[:, 48:96], T.PT[:, 0:48], deps=[m1, m2])
+    lsh = [ts(T.LSH[:, k:k + 1], T.SHN[:, p:p + 1], T.P48[:, :], A.add, deps=[d_sh, c_48]) for k, p in enumerate(dest)]
     nn = tt(T.NN[:, :], T.WT[:, :].indirect(T.LP[:, 0:12]), T.CI[:, :], A.add, deps=lp + [wt1, wt2] + c_ci)
     r1 = cp(T.R1[:, :], T.NN[:, 0:96].indirect(T.LSH[:, 0:3]), deps=[nn] + lsh)
-    r2 = cp(T.R2[:, :], T.NN[:, 96:192].indirect(T.LSH[:, 0:3]), deps=[nn] + lsh)
+    r2 = ac(T.R2[:, :], T.NN[:, 96:192].indirect(T.LSH[:, 0:3]), deps=[nn] + lsh)
     la = [cp(T.LA[:, 0::3], T.R1[:, 0::2], deps=[r1]), cp(T.LA[:, 2::3], T.R1[:, 1::2], deps=[r1])]
     k1 = tt(T.K1[:, :], T.R2[:, 0::2], T.R2[:, 1::2], A.add, deps=[r2])
     la.append(cp(T.LA[:, 1::3], T.K1[:, :], deps=[k1]))
@@ -147,59 +154,38 @@ def rank_program(g, core, T, topo):
         sa.append([cp(T.SA[:, a:b], T.X[:, :].indirect(T.LA[:, 24 * k:24 * k + 12]), deps=la + [d_x]),
                    ac(T.SA[:, b:a + SLW], T.X[:, :].indirect(T.LA[:, 24 * k + 12:24 * k + 24]), deps=la + [d_x])])
 
-    def addr(p):
-        return topo.addr(T.cores[p], core)
-
-    def transfer(p, buf, win, k, es, arr):
-        rid, pid = addr(p)
+    def transfer(p, srcs, win, es, arr, alu=0):
+        rid, pid = topo.addr(T.cores[p], core)
         c = place(r, p)
-        return RemoteDMATransfer(src=buf[:, SLW * k:SLW * k + SLW], dst=win[:, c:c + SLW], dst_ids=[DstId(rid=rid, pnc=pid)],
-                                 dma_engine_mask=bits(es), remote_sem=T.sem[arr])
+        return RemoteDMATransfer(srcs=srcs, dsts=[win[:, c:c + SLW]], dst_ids=[DstId(rid=rid, pnc=pid)],
+                                 dma_engine_mask=bits(es), remote_sem=T.sem[arr], alu_op=alu)
 
-    def send(p, buf, win, k, es, arr, deps):
-        rid, pid = addr(p)
-        c = place(r, p)
-        return op("g", lambda: g.remote_dma(win[:, c:c + SLW], buf[:, SLW * k:SLW * k + SLW], T.sem[arr], T.sem["left"], pid, rid,
-                                            bits(es)), deps, "r")
+    def send(transfers, deps):
+        return op("g", lambda: g.remote_dma_fused(transfers, local_sem=T.sem["left"]), deps, "r")
 
-    left = [0]
     half = [feng[:len(feng) // 2], feng[len(feng) // 2:]]
-    got0 = {}
-    op("g", lambda: g.remote_dma_fused([transfer(p, T.SA, T.W0, k, half[k], "arr0_%d" % r) for k, p in enumerate(far)],
-                                       local_sem=T.sem["left"]), sa[0] + sa[1], "r")
-    send(near[0], T.SA, T.W0, 2, neng, "arr0_%d" % r, sa[2])
-    left[0] += len(feng) + len(neng)
+    send([transfer(p, [T.SA[:, SLW * k:SLW * k + SLW]], T.W0, half[k], "arr0_%d" % r) for k, p in enumerate(far)], sa[0] + sa[1])
+    send([transfer(near[0], [T.SA[:, 2 * SLW:3 * SLW]], T.W0, neng, "arr0_%d" % r)], sa[2])
+    left = [len(feng) + len(neng)]
     arr0 = [("sem", "arr0_%d" % q, len(half[0]) if q in far else len(neng)) for q in others]
 
-    r8b = cp(T.R8B[:, :], T.R8[:, :], deps=[d_r8])
-    b2 = ts(T.BO2[:, :], T.BO[:, :], 4, A.arith_shift_right, deps=[i_b])
-    bn = ts(T.BN[:, :], T.BO2[:, :], 0, A.is_equal, deps=[b2])
-    pr = [op("t", lambda: t.matmul(T.PR[:, 0:288], T.BN[:, :], T.R8B[:, 0:288], True, True), [bn, r8b]),
-          op("t", lambda: t.matmul(T.PR[:, 512:800], T.BN[:, :], T.R8B[:, 288:576], True, True), [bn, r8b])]
     nbu = cp(T.NBU[:, :], T.NB[:, :], deps=[d_nb])
-    rel = [ac(T.REL[:, 0:288], T.PR[:, 0:288], deps=[pr[0]]), ac(T.REL[:, 288:576], T.PR[:, 512:800], deps=[pr[1]])]
     ow = [cp(T.OWN[:, 0::3], T.NN[:, 0:48:2], deps=[nn]), cp(T.OWN[:, 2::3], T.NN[:, 49:96:2], deps=[nn])]
     ko = tt(T.KO[:, :], T.NN[:, 96:144:2], T.NN[:, 145:192:2], A.add, deps=[nn])
     acf = cp(T.ACF[:, 0:3], T.AC[:, 0:3], deps=[d_ac])
     ow.append(cp(T.OWN[:, 1::3], T.KO[:, :], deps=[ko]))
-    im2 = ts(T.IM2[:, :], T.IM[:, :], 15, A.bitwise_and, deps=[i_m])
-    npc = ts(T.NP[:, :], T.N4[:, :], T.P192[:, :], A.add, deps=[i_n, c_192])
-    p24 = ts(T.P24[:, :], T.N4[:, :], 0, A.mult, T.P48[:, :], A.add, deps=[i_n, c_48])
-    mk = ts(T.MK[:, :], T.IM2[:, :], 0, A.is_equal, deps=[im2])
     shf = cp(T.SHF[:, :], T.SHN[:, :], deps=[d_sh])
-    p24 = ts(T.P24[:, :], T.P24[:, :], 0.5, A.mult, deps=[p24])
     lsz = [ts(T.LSZ[:, 4 * k:4 * k + 4], T.NP[:, :], T.SHF[:, p:p + 1], A.add, deps=[npc, shf]) for k, p in enumerate(dest)]
     arm = [ac(T.ARM[:, 192 * k:192 * k + 192], T.AT[:, :].indirect(T.NBU[:, :]), deps=i_a + [nbu] + [c_lo, c_hi],
               scale=[None, None, T.LO[:, :], T.HI[:, :]][k]) for k in range(4)]
     own0 = ac(T.W0[:, 0:OWNW], T.X[:, :].indirect(T.OWN[:, :]), deps=ow + [d_x])
-    arx = [ac(T.ARX[:, 0::2], T.ARM[:, 384:576:2], deps=[arm[2]]), ac(T.ARX[:, 1::2], T.ARM[:, 577:768:2], deps=[arm[3]])]
 
     def level(lst, ldeps, tmp, out):
         m = tt(tmp[:, :], T.REL[:, :].indirect(lst[:, 0:3]), T.MK[:, :], A.mult, deps=rel + [mk] + ldeps)
         return [op("v", lambda c=c: v.tensor_reduce(out[:, c:c + 1], tmp[:, 16 * c:16 * c + 16], AxisListType.X, A.add), [m])
                 for c in range(3)]
 
-    idc = ts(T.ID24[:, :], T.REL[:, 0:1], 24, A.mult, deps=[rel[0]])
+    idc = ts(T.ID24[:, :], T.REL[:, 0:1], 24, A.mult, deps=rel)
     l1 = ts(T.L1[:, 0:3], T.PO[:, 0:3], T.ID24[:, :], A.add, deps=[idc, d_po])
     wv = level(T.L1, [l1], T.M1, T.WV)
     l2 = [ts(T.L2[:, c:c + 1], T.WV[:, c:c + 1], 24, A.mult, T.ACF[:, c:c + 1], A.add, deps=wv + [acf]) for c in range(3)]
@@ -208,14 +194,40 @@ def rank_program(g, core, T, topo):
     ev = level(T.L3, l3, T.M3, T.EV)
     le = [ts(T.LE[:, c::3], T.T16[:, :], T.EV[:, c:c + 1], A.add, deps=[i_t] + ev) for c in range(3)]
     zz = tt(T.ZZ[:, :], T.WT[:, :].indirect(T.LE[:, :]), T.ARM[:, :], A.add, deps=le + arm)
-    zs1 = cp(T.ZS1[:, :], T.ZZ[:, 0:384].indirect(T.LSZ[:, :]), deps=[zz] + lsz)
-    zs2 = cp(T.ZS2[:, :], T.ZZ[:, 384:768].indirect(T.LSZ[:, :]), deps=[zz] + lsz)
-    lb = [cp(T.LB[:, 0::3], T.ZS1[:, 0::2], deps=[zs1]), cp(T.LB[:, 2::3], T.ZS1[:, 1::2], deps=[zs1])]
-    kb = tt(T.KB[:, :], T.ZS2[:, 0::2], T.ZS2[:, 1::2], A.add, deps=[zs2])
+    zs1 = ac(T.ZS1[:, :], T.ZZ[:, 0:384].indirect(T.LSZ[:, :]), deps=[zz] + lsz)
+    zs2 = ac(T.ZS2[:, :], T.ZZ[:, 384:768].indirect(T.LSZ[:, :]), deps=[zz] + lsz)
+    arx = [ac(T.ARX[:, 0::2], T.ARM[:, 384:576:2], deps=[arm[2]]), ac(T.ARX[:, 1::2], T.ARM[:, 577:768:2], deps=[arm[3]])]
     kc = tt(T.KC[:, :], T.ZZ[:, 384:576:2], T.ZZ[:, 577:768:2], A.add, deps=[zz])
-    lb.append(cp(T.LB[:, 1::3], T.KB[:, :], deps=[kb]))
     lc = [cp(T.LC[:, 0::3], T.ZZ[:, 0:192:2], deps=[zz]), cp(T.LC[:, 2::3], T.ZZ[:, 193:384:2], deps=[zz]),
           cp(T.LC[:, 1::3], T.KC[:, :], deps=[kc])]
+    lb = [cp(T.LB[:, 0::3], T.ZS1[:, 0::2], deps=[zs1]), cp(T.LB[:, 2::3], T.ZS1[:, 1::2], deps=[zs1])]
+    kb = tt(T.KB[:, :], T.ZS2[:, 0::2], T.ZS2[:, 1::2], A.add, deps=[zs2])
+    lb.append(cp(T.LB[:, 1::3], T.KB[:, :], deps=[kb]))
+    ley = [ts(T.LEY[:, c::3], T.P24[:, :], T.VV[:, c:c + 1], A.add, deps=vv + [p24]) for c in range(3)]
+    zy1 = tt(T.ZY1[:, :], T.WT[:, 0:48].indirect(T.LEY[:, :]), T.ARM[:, 0:192], A.add, deps=ley + arm)
+    zy2 = tt(T.ZY2[:, :], T.WT[:, 48:96].indirect(T.LEY[:, :]), T.ARX[:, :], A.add, deps=ley + arx)
+    ly = [cp(T.LY[:, 0::3], T.ZY1[:, 0::2], deps=[zy1]), cp(T.LY[:, 2::3], T.ZY1[:, 1::2], deps=[zy1])]
+    ky = tt(T.KY[:, :], T.ZY2[:, 0::2], T.ZY2[:, 1::2], A.add, deps=[zy2])
+    ly.append(cp(T.LY[:, 1::3], T.KY[:, :], deps=[ky]))
+
+    for k, p in enumerate(dest):
+        src = [T.W0[:, :].indirect(T.LB[:, 96 * k + 24 * n:96 * k + 24 * n + 24]) for n in range(4)]
+        f0, f1, f2, f3 = [T[x][:, SLW * k:SLW * k + SLW] for x in ("F0", "F1", "F2", "F3")]
+        deps = lb + [own0] + arr0
+        x2 = ac(f2, src[2], deps)
+        x3 = ac(f3, src[3], deps)
+        if k == 0:
+            x0 = cp(f0, src[0], deps)
+            x1 = tt(f1, src[1], f0, A.max, deps + [x0])
+            parts, last = [f1, f2, f3], [x1, x2, x3]
+        else:
+            x0 = tt(f0, src[0], f2, A.max, deps + [x2])
+            x1 = tt(f1, src[1], f0, A.max, deps + [x0])
+            parts, last = [f1, f3], [x1, x3]
+        es = feng if p in far else neng
+        send([transfer(p, parts, T.W1, es, "arr1_%d" % r, 2)], last)
+        left[0] += len(es)
+    arr1 = [("sem", "arr1_%d" % q, len(feng) if q in far else len(neng)) for q in others]
 
     pc = [T.PC0, T.PC1, T.PC2]
     last_merge = [None, None, None]
@@ -231,11 +243,10 @@ def rank_program(g, core, T, topo):
         src = [win[:, :].indirect(x) for x in lists]
         free = [last_merge[b]] if last_merge[b] is not None else []
         if first:
-            H0 = T.H0[:, first - 512:first - 512 + width]
             g3 = ac(G3, src[3], deps)
             p3 = ac(P, G3, [g3] + free)
-            h0 = cp(H0, src[0], deps)
-            h1 = tt(H1, src[1], H0, A.max, deps + [h0])
+            h0 = cp(T.H0[:, 0:width], src[0], deps)
+            h1 = tt(H1, src[1], T.H0[:, 0:width], A.max, deps + [h0])
             h2 = tt(H2, src[2], H1, A.max, deps + [h1])
         else:
             g2 = ac(G2, src[2], deps)
@@ -247,30 +258,16 @@ def rank_program(g, core, T, topo):
         last_merge[b] = res
         return res
 
-    for k, p in enumerate(dest):
-        x = piece(T.W0, [T.LB[:, 96 * k + 24 * n:96 * k + 24 * n + 24] for n in range(4)], SLW, T.SB[:, SLW * k:SLW * k + SLW],
-                  lb + [own0] + arr0, 512 if k == 0 else 0)
-        es = feng if p in far else neng
-        send(p, T.SB, T.W1, k, es, "arr1_%d" % r, [x])
-        left[0] += len(es)
-    arr1 = [("sem", "arr1_%d" % q, len(feng) if q in far else len(neng)) for q in others]
     own1 = []
     for k in range(3):
         own1.append(piece(T.W0, [T.LC[:, 72 * n + 24 * k:72 * n + 24 * k + 24] for n in range(4)], SLW,
-                          T.W1[:, SLW * k:SLW * k + SLW], lc + [own0] + arr0, 0))
-
-    ley = [ts(T.LEY[:, c::3], T.P24[:, :], T.VV[:, c:c + 1], A.add, deps=vv + [p24]) for c in range(3)]
-    zy1 = tt(T.ZY1[:, :], T.WT[:, 0:48].indirect(T.LEY[:, :]), T.ARM[:, 0:192], A.add, deps=ley + arm)
-    zy2 = tt(T.ZY2[:, :], T.WT[:, 48:96].indirect(T.LEY[:, :]), T.ARX[:, :], A.add, deps=ley + arx)
-    ly = [cp(T.LY[:, 0::3], T.ZY1[:, 0::2], deps=[zy1]), cp(T.LY[:, 2::3], T.ZY1[:, 1::2], deps=[zy1])]
-    ky = tt(T.KY[:, :], T.ZY2[:, 0::2], T.ZY2[:, 1::2], A.add, deps=[zy2])
-    ly.append(cp(T.LY[:, 1::3], T.KY[:, :], deps=[ky]))
+                          T.W1[:, SLW * k:SLW * k + SLW], lc + [own0] + arr0, False))
 
     stores, a = [], 0
     for k, nodes in enumerate((16, 20, 12)):
         c0, cw = a // 2 * 3, nodes // 2 * 3
         x = piece(T.W1, [T.LY[:, 72 * n + c0:72 * n + c0 + cw] for n in range(4)], nodes * 24,
-                  T.YB[:, a * 24:(a + nodes) * 24], ly + own1 + arr1, 1024 if k == 0 else 0)
+                  T.YB[:, a * 24:(a + nodes) * 24], ly + own1 + arr1, k == 0)
         stores.append(ld("y", T.y[:, a * 24:(a + nodes) * 24], T.YB[:, a * 24:(a + nodes) * 24], [x]))
         a += nodes
     op("y", None, stores, "w")
@@ -281,14 +278,23 @@ def rank_program(g, core, T, topo):
         for d in o["deps"]:
             if not isinstance(d, tuple):
                 users[d].append(o["q"])
-    names, made = {}, [0]
+    names, made, total, gname = {}, [0], {}, {}
+    for k, o in enumerate(ops):
+        if o["grp"]:
+            total[o["grp"]] = total.get(o["grp"], 0) + (16 if o["kind"] == "d" else 1)
     for k, o in enumerate(ops):
         if o["kind"] in "cd" and users[k]:
             if o["kind"] == "c" and all(q == o["q"] for q in users[k]):
-                names[k] = ("self_" + o["q"], 0)
-            else:
-                names[k] = ("x%d" % made[0], 16 if o["kind"] == "d" else 1)
+                names[k] = ("self_" + o["q"], 0, 0)
+                continue
+            inc = 16 if o["kind"] == "d" else 1
+            name = gname.get(o["grp"])
+            if name is None:
+                name = "x%d" % made[0]
                 made[0] += 1
+                if o["grp"]:
+                    gname[o["grp"]] = name
+            names[k] = (name, inc, total.get(o["grp"], inc))
     done = {q: {} for q in queues}
     count = {q: 0 for q in queues}
 
@@ -305,7 +311,7 @@ def rank_program(g, core, T, topo):
             elif names[d][1] == 0:
                 wait(q, names[d][0], count[q])
             else:
-                wait(q, names[d][0], names[d][1])
+                wait(q, names[d][0], names[d][2])
         if o["kind"] == "w":
             continue
         ins = o["f"]()
@@ -314,7 +320,7 @@ def rank_program(g, core, T, topo):
                 count[q] += 1
                 ins.then_inc(T.sem[names[k][0]], 1)
             else:
-                ins.then_inc(T.sem[names[k][0]], names[k][1])
+                ins.then_inc(T.sem[names[k][0]], names[k][2] if False else names[k][1])
     for q in queues:
         if count[q]:
             wait(q, "self_" + q, count[q])

@@ -1,29 +1,31 @@
 from concourse.bass import DstId, RemoteDMATransfer
 from concourse.mybir import AluOpType, AxisListType, ActivationFunctionType
 
-NX = 110
+NX = 130
 SCRATCH = {
     "X": ("sbuf", [128, 1152], "float32"), "TR": ("sbuf", [128, 48], "int32"), "PO": ("sbuf", [128, 4], "int32"),
     "SHN": ("sbuf", [128, 4], "int32"), "NB": ("sbuf", [128, 12], "int32"), "AC": ("sbuf", [128, 4], "int32"),
-    "REL": ("sbuf", [128, 576], "int32"),
-    "IP": ("sbuf", [128, 2], "int32"), "DD": ("sbuf", [128, 128], "float32"), "IM": ("sbuf", [128, 48], "int32"),
-    "IM2": ("sbuf", [128, 48], "int32"),
+    "IP": ("sbuf", [128, 2], "int32"), "DD": ("sbuf", [128, 128], "float32"), "GI": ("sbuf", [128, 128], "float32"),
+    "IM": ("sbuf", [128, 48], "int32"), "IM2": ("sbuf", [128, 48], "int32"),
     "CI": ("sbuf", [128, 192], "float32"), "C48": ("sbuf", [128, 96], "float32"), "T16": ("sbuf", [128, 16], "float32"),
     "N4": ("sbuf", [128, 4], "float32"), "AT": ("sbuf", [128, 112], "float32"),
-    "B1": ("sbuf", [128, 2], "int32"), "B8": ("sbuf", [128, 2], "int32"), "LO": ("sbuf", [128, 1], "float32"),
+    "B1": ("sbuf", [128, 2], "int32"), "B8": ("sbuf", [128, 2], "int32"), "BQ": ("sbuf", [128, 2], "int32"),
+    "BG": ("sbuf", [128, 2], "int32"), "PG": ("sbuf", [128, 1], "float32"), "U2": ("sbuf", [128, 2], "float32"),
+    "LO": ("sbuf", [128, 1], "float32"),
     "HI": ("sbuf", [128, 1], "float32"), "P48": ("sbuf", [128, 1], "float32"), "P192": ("sbuf", [128, 1], "float32"),
     "P24C": ("sbuf", [128, 1], "float32"), "P24": ("sbuf", [128, 4], "float32"),
-    "SH": ("sbuf", [128, 128], "bfloat16"), "SL": ("sbuf", [128, 128], "bfloat16"),
+    "SH": ("sbuf", [128, 128], "bfloat16"), "SL": ("sbuf", [128, 128], "bfloat16"), "ON": ("sbuf", [128, 128], "bfloat16"),
     "MK": ("sbuf", [128, 48], "float32"), "NP": ("sbuf", [128, 4], "float32"),
     "TRB": ("sbuf", [128, 48], "bfloat16"), "WT": ("sbuf", [128, 96], "float32"), "LP": ("sbuf", [128, 12], "uint16"),
     "NN": ("sbuf", [128, 192], "float32"), "LSH": ("sbuf", [128, 4], "uint16"), "SHF": ("sbuf", [128, 4], "float32"),
     "R1": ("sbuf", [128, 48], "float32"), "R2": ("sbuf", [128, 48], "float32"), "K1": ("sbuf", [128, 24], "float32"),
     "LA": ("sbuf", [128, 72], "uint16"), "KO": ("sbuf", [128, 24], "float32"), "OWN": ("sbuf", [128, 72], "uint16"),
-    "NBU": ("sbuf", [128, 12], "uint16"),
-    "ACF": ("sbuf", [128, 4], "float32"), "ID24": ("sbuf", [128, 1], "float32"),
-    "L1": ("sbuf", [128, 4], "uint16"), "L2": ("sbuf", [128, 4], "uint16"), "L3": ("sbuf", [128, 4], "uint16"),
-    "M1": ("sbuf", [128, 48], "float32"), "M2": ("sbuf", [128, 48], "float32"), "M3": ("sbuf", [128, 48], "float32"),
-    "WV": ("sbuf", [128, 4], "float32"), "VV": ("sbuf", [128, 4], "float32"), "EV": ("sbuf", [128, 4], "float32"),
+    "NBU": ("sbuf", [128, 12], "uint16"), "IT": ("sbuf", [128, 16], "float32"), "IDC": ("sbuf", [128, 1], "float32"),
+    "EQ": ("sbuf", [128, 2], "float32"), "MW": ("sbuf", [128, 96], "float32"),
+    "LM": ("sbuf", [128, 6], "uint16"), "LV": ("sbuf", [128, 6], "uint16"),
+    "P1": ("sbuf", [128, 96], "bfloat16"), "P2": ("sbuf", [128, 96], "bfloat16"), "P3": ("sbuf", [128, 96], "bfloat16"),
+    "M2": ("sbuf", [128, 48], "float32"), "M3": ("sbuf", [128, 48], "float32"),
+    "VV": ("sbuf", [128, 4], "float32"), "EV": ("sbuf", [128, 4], "float32"),
     "LE": ("sbuf", [128, 48], "uint16"), "ARM": ("sbuf", [128, 768], "float32"), "ARX": ("sbuf", [128, 192], "float32"),
     "ZZ": ("sbuf", [128, 768], "float32"), "LSZ": ("sbuf", [128, 12], "uint16"),
     "ZS1": ("sbuf", [128, 192], "float32"), "ZS2": ("sbuf", [128, 192], "float32"), "KB": ("sbuf", [128, 96], "float32"),
@@ -35,12 +37,11 @@ SCRATCH = {
     "F0": ("sbuf", [128, 1152], "float32"), "F1": ("sbuf", [128, 1152], "float32"),
     "F2": ("sbuf", [128, 1152], "float32"), "F3": ("sbuf", [128, 1152], "float32"),
     "G2": ("sbuf", [128, 2304], "float32"), "G3": ("sbuf", [128, 2304], "float32"),
-    "H0": ("sbuf", [128, 512], "float32"), "H1": ("sbuf", [128, 2304], "float32"), "H2": ("sbuf", [128, 2304], "float32"),
-    "PT": ("psum", [128, 512], "float32"),
+    "H0": ("sbuf", [128, 2304], "float32"), "H1": ("sbuf", [128, 2304], "float32"), "H2": ("sbuf", [128, 2304], "float32"),
+    "PT": ("psum", [128, 512], "float32"), "PW": ("psum", [128, 512], "float32"),
     "PC0": ("psum", [128, 512], "float32"), "PC1": ("psum", [128, 512], "float32"), "PC2": ("psum", [128, 512], "float32"),
 }
-SEMAPHORES = (["self_v", "self_s", "self_t", "self_g", "self_y", "left"] + ["arr%d_%d" % (t, q) for t in range(2) for q in range(4)]
-              + ["x%d" % k for k in range(NX)])
+SEMAPHORES = ["left"] + ["arr%d_%d" % (t, q) for t in range(2) for q in range(4)] + ["x%d" % k for k in range(NX)]
 OWNW, SLW = 48 * 24, 16 * 24
 
 
@@ -55,9 +56,14 @@ def rank_program(g, core, T, topo):
     A, ACT = AluOpType, ActivationFunctionType
     ops = []
 
-    def op(q, f, deps=(), kind="c", grp=None):
-        ops.append({"q": q, "f": f, "deps": list(deps), "kind": kind, "grp": grp})
+    def op(q, f, deps=(), kind="c"):
+        ops.append({"q": q, "f": f, "deps": list(deps), "kind": kind, "grp": len(ops)})
         return len(ops) - 1
+
+    def join(*ks):
+        for k in ks:
+            ops[k]["grp"] = ks[0]
+        return list(ks)
 
     v, s, t = g.vector, g.scalar, g.tensor
     queues = {"v": v, "s": s, "t": t, "g": g, "y": g.sync}
@@ -78,8 +84,11 @@ def rank_program(g, core, T, topo):
             return op("s", lambda: s.activation(out, a, ACT.Copy), deps)
         return op("s", lambda: s.activation(out, a, ACT.Identity, scale=scale), deps)
 
-    def ld(q, out, in_, deps=(), grp=None):
-        return op(q, lambda: queues[q].dma_start(out, in_), deps, "d", grp)
+    def mm(out, lhs, rhs, start, stop, deps):
+        return op("t", lambda: t.matmul(out, lhs, rhs, start, stop), deps)
+
+    def ld(q, out, in_, deps=()):
+        return op(q, lambda: queues[q].dma_start(out, in_), deps, "d")
 
     others = [p for p in range(len(T.cores)) if p != r]
     near = [p for p in others if T.cores[p] in topo.cores_of(core)]
@@ -97,9 +106,9 @@ def rank_program(g, core, T, topo):
     d_rd = ld("y", T.TR[:, 24:48], T.rel[:, 192:576])
     d_sh = ld("s", T.SHN[:, 0:4], T.shown[:, :])
     d_x = ld("s", T.X[:, :], T.x[:, :])
-    d_nb = ld("y", T.NB[:, 0:12], T.nbr[:, :])
     d_ac = ld("y", T.AC[:, 0:3], T.act[:, :])
-    rel = [ld("y", T.REL[q::16, :], T.rel[:, :], [d_rd], "rel") for q in range(16)]
+    d_nb = ld("y", T.NB[:, 0:12], T.nbr[:, :])
+    join(d_ra, d_rd)
 
     def iota(out, pat, base, cm, f32=True):
         if f32:
@@ -111,48 +120,65 @@ def rank_program(g, core, T, topo):
     i_c = iota(T.C48[:, :], [[0, 2], [24, 48]], 0, 0)
     i_m = iota(T.IM[:, :], [[0, 3], [1, 16]], 0, -1, False)
     i_n = iota(T.N4[:, :], [[48, 4]], 0, 0)
+    i_g = iota(T.GI[:, :], [[1, 8], [0, 16]], 0, 0)
     i_t = iota(T.T16[:, :], [[24, 4], [0, 4]], 0, 0)
     hole = 48 + 16 * r + 16
     i_a = [iota(T.AT[:, 0:hole], [[24, hole]], 0, 0)]
     if hole < 112:
         i_a.append(iota(T.AT[:, hole:112], [[24, 112 - hole]], 24 * (hole - 16), 0))
+    join(*i_a)
 
-    c_1 = ts(T.B1[:, :], T.IP[:, :], 1, A.bitwise_and, deps=[i_p])
-    c_8 = ts(T.B8[:, :], T.IP[:, :], 8, A.bitwise_and, deps=[i_p])
-    c_lo = ts(T.LO[:, :], T.B8[:, 0:1], 0, A.is_equal, deps=[c_1, c_8])
-    c_hi = ts(T.HI[:, :], T.B8[:, 0:1], 0, A.is_gt, deps=[c_8])
-    c_48 = ts(T.P48[:, :], T.B1[:, 0:1], 48, A.mult, deps=[c_1])
-    c_192 = ts(T.P192[:, :], T.B1[:, 0:1], 192, A.mult, deps=[c_1])
-    c_24 = ts(T.P24C[:, :], T.B1[:, 0:1], 24, A.mult, deps=[c_1])
-    c_sh = ts(T.SH[:, :], T.DD[:, :], -8, A.is_equal, T.HI[:, :], A.mult, deps=[i_d, c_hi])
-    c_sl = ts(T.SL[:, :], T.DD[:, :], 8, A.is_equal, T.LO[:, :], A.mult, deps=[i_d, c_lo])
-    c_ci = [cp(T.CI[:, 0:96], T.C48[:, :], deps=[i_c]),
-            ts(T.CI[:, 96:144], T.C48[:, 0:48], T.LO[:, :], A.mult, deps=[i_c, c_lo]),
-            ts(T.CI[:, 144:192], T.C48[:, 0:48], T.HI[:, :], A.mult, deps=[i_c, c_hi])]
+    c_b = join(ts(T.B1[:, :], T.IP[:, :], 1, A.bitwise_and, deps=[i_p]),
+               ts(T.B8[:, :], T.IP[:, :], 8, A.bitwise_and, deps=[i_p]),
+               ts(T.BQ[:, :], T.IP[:, :], 15, A.bitwise_and, deps=[i_p]),
+               ts(T.BG[:, :], T.IP[:, :], 4, A.arith_shift_right, deps=[i_p]))
+    c_m = join(ts(T.LO[:, :], T.B8[:, 0:1], 0, A.is_equal, deps=c_b),
+               ts(T.HI[:, :], T.B8[:, 0:1], 0, A.is_gt, deps=c_b),
+               ts(T.P48[:, :], T.B1[:, 0:1], 48, A.mult, deps=c_b),
+               ts(T.P192[:, :], T.B1[:, 0:1], 192, A.mult, deps=c_b),
+               ts(T.P24C[:, :], T.B1[:, 0:1], 24, A.mult, deps=c_b),
+               cp(T.PG[:, :], T.BG[:, 0:1], deps=c_b),
+               ts(T.U2[:, 0:1], T.BQ[:, 0:1], 1, A.add, deps=c_b))
+    c_s = join(ts(T.SH[:, :], T.DD[:, :], -8, A.is_equal, T.HI[:, :], A.mult, deps=[i_d] + c_m),
+               ts(T.SL[:, :], T.DD[:, :], 8, A.is_equal, T.LO[:, :], A.mult, deps=[i_d] + c_m))
+    c_u = ts(T.U2[:, 1:2], T.BQ[:, 0:1], 9, A.add, T.HI[:, :], A.mult, deps=c_b + c_m)
+    c_ci = join(cp(T.CI[:, 0:96], T.C48[:, :], deps=[i_c]),
+                ts(T.CI[:, 96:144], T.C48[:, 0:48], T.LO[:, :], A.mult, deps=[i_c] + c_m),
+                ts(T.CI[:, 144:192], T.C48[:, 0:48], T.HI[:, :], A.mult, deps=[i_c] + c_m))
     im2 = ts(T.IM2[:, :], T.IM[:, :], 15, A.bitwise_and, deps=[i_m])
-    npc = ts(T.NP[:, :], T.N4[:, :], T.P192[:, :], A.add, deps=[i_n, c_192])
-    p24 = ts(T.P24[:, :], T.N4[:, :], 0, A.mult, T.P24C[:, :], A.add, deps=[i_n, c_24])
+    c_n = join(ts(T.NP[:, :], T.N4[:, :], T.P192[:, :], A.add, deps=[i_n] + c_m),
+               ts(T.P24[:, :], T.N4[:, :], 0, A.mult, T.P24C[:, :], A.add, deps=[i_n] + c_m))
     mk = ts(T.MK[:, :], T.IM2[:, :], 0, A.is_equal, deps=[im2])
+    on = ts(T.ON[:, :], T.GI[:, :], T.PG[:, :], A.is_equal, deps=[i_g] + c_m)
 
     trb = cp(T.TRB[:, :], T.TR[:, :], deps=[d_ra, d_rd])
-    m1 = op("t", lambda: t.matmul(T.PT[:, 0:24], T.SH[:, :], T.TRB[:, 24:48], True, True), [trb, c_sh])
-    m2 = op("t", lambda: t.matmul(T.PT[:, 24:48], T.SL[:, :], T.TRB[:, 0:24], True, True), [trb, c_sl])
+    m1 = mm(T.PT[:, 0:24], T.SH[:, :], T.TRB[:, 24:48], True, True, [trb] + c_s)
+    m2 = mm(T.PT[:, 24:48], T.SL[:, :], T.TRB[:, 0:24], True, True, [trb] + c_s)
+    join(m1, m2)
     wt1 = cp(T.WT[:, 0:48], T.TR[:, :], deps=[d_ra, d_rd])
-    lp = [ts(T.LP[:, 3 * k:3 * k + 3], T.PO[:, 0:3], 24 * k, A.add, deps=[d_po]) for k in range(4)]
+    lp = join(*[ts(T.LP[:, 3 * k:3 * k + 3], T.PO[:, 0:3], 24 * k, A.add, deps=[d_po]) for k in range(4)])
     wt2 = cp(T.WT[:, 48:96], T.PT[:, 0:48], deps=[m1, m2])
-    lsh = [ts(T.LSH[:, k:k + 1], T.SHN[:, p:p + 1], T.P48[:, :], A.add, deps=[d_sh, c_48]) for k, p in enumerate(dest)]
+    lsh = join(*[ts(T.LSH[:, k:k + 1], T.SHN[:, p:p + 1], T.P48[:, :], A.add, deps=[d_sh] + c_m) for k, p in enumerate(dest)])
     nn = tt(T.NN[:, :], T.WT[:, :].indirect(T.LP[:, 0:12]), T.CI[:, :], A.add, deps=lp + [wt1, wt2] + c_ci)
+    idt = tt(T.IT[:, :], T.WT[:, 0:16], T.MK[:, 0:16], A.mult, deps=[wt1, mk])
     r1 = cp(T.R1[:, :], T.NN[:, 0:96].indirect(T.LSH[:, 0:3]), deps=[nn] + lsh)
     r2 = ac(T.R2[:, :], T.NN[:, 96:192].indirect(T.LSH[:, 0:3]), deps=[nn] + lsh)
+    idc = op("v", lambda: v.tensor_reduce(T.IDC[:, :], T.IT[:, :], AxisListType.X, A.add), [idt])
     la = [cp(T.LA[:, 0::3], T.R1[:, 0::2], deps=[r1]), cp(T.LA[:, 2::3], T.R1[:, 1::2], deps=[r1])]
     k1 = tt(T.K1[:, :], T.R2[:, 0::2], T.R2[:, 1::2], A.add, deps=[r2])
+    eq = ts(T.EQ[:, :], T.U2[:, :], T.IDC[:, :], A.subtract, 1, A.is_equal, deps=[idc, c_u] + c_m)
     la.append(cp(T.LA[:, 1::3], T.K1[:, :], deps=[k1]))
+    join(*la)
+    p1 = join(*[ts(T.P1[:, 48 * k:48 * k + 48], T.WT[:, 24 * k:24 * k + 24].indirect(T.LP[:, 0:3]), T.EQ[:, k:k + 1], A.mult,
+                   deps=lp + [wt1, eq]) for k in range(2)])
 
     sa = []
     for k in range(3):
         a, b = SLW * k, SLW * k + SLW // 2
         sa.append([cp(T.SA[:, a:b], T.X[:, :].indirect(T.LA[:, 24 * k:24 * k + 12]), deps=la + [d_x]),
                    ac(T.SA[:, b:a + SLW], T.X[:, :].indirect(T.LA[:, 24 * k + 12:24 * k + 24]), deps=la + [d_x])])
+    join(*(sa[0] + sa[1]))
+    join(*sa[2])
 
     def transfer(p, srcs, win, es, arr, alu=0):
         rid, pid = topo.addr(T.cores[p], core)
@@ -169,158 +195,147 @@ def rank_program(g, core, T, topo):
     left = [len(feng) + len(neng)]
     arr0 = [("sem", "arr0_%d" % q, len(half[0]) if q in far else len(neng)) for q in others]
 
+    def added(c, part, deps):
+        return join(mm(T.PW[:, c:c + 48], T.ON[:, :], part[:, 0:48], True, False, deps + [on]),
+                    mm(T.PW[:, c:c + 48], T.ON[:, :], part[:, 48:96], False, True, deps + [on]))
+
+    def as_list(out, tmp, m):
+        return join(*[op("v", lambda c=c: v.tensor_reduce(out[:, c:c + 1], tmp[:, 16 * c:16 * c + 16], AxisListType.X, A.add), [m])
+                      for c in range(3)])
+
+    qw = added(0, T.P1, p1)
     nbu = cp(T.NBU[:, :], T.NB[:, :], deps=[d_nb])
+    lm = join(*[ts(T.LM[:, 3 * k:3 * k + 3], T.AC[:, 0:3], 24 * k, A.add, deps=[d_ac]) for k in range(2)])
+    mw = join(*[ts(T.MW[:, 48 * k:48 * k + 48], T.PW[:, 0:48], 1, A.add, T.U2[:, k:k + 1], A.is_equal, deps=qw + [c_u] + c_m)
+                for k in range(2)])
     ow = [cp(T.OWN[:, 0::3], T.NN[:, 0:48:2], deps=[nn]), cp(T.OWN[:, 2::3], T.NN[:, 49:96:2], deps=[nn])]
     ko = tt(T.KO[:, :], T.NN[:, 96:144:2], T.NN[:, 145:192:2], A.add, deps=[nn])
-    acf = cp(T.ACF[:, 0:3], T.AC[:, 0:3], deps=[d_ac])
+    p2 = tt(T.P2[:, :], T.WT[:, 0:48].indirect(T.LM[:, :]), T.MW[:, :], A.mult, deps=lm + mw + [wt1])
+    qv = added(48, T.P2, [p2])
     ow.append(cp(T.OWN[:, 1::3], T.KO[:, :], deps=[ko]))
+    join(*ow)
     shf = cp(T.SHF[:, :], T.SHN[:, :], deps=[d_sh])
-    lsz = [ts(T.LSZ[:, 4 * k:4 * k + 4], T.NP[:, :], T.SHF[:, p:p + 1], A.add, deps=[npc, shf]) for k, p in enumerate(dest)]
-    arm = [ac(T.ARM[:, 192 * k:192 * k + 192], T.AT[:, :].indirect(T.NBU[:, :]), deps=i_a + [nbu] + [c_lo, c_hi],
-              scale=[None, None, T.LO[:, :], T.HI[:, :]][k]) for k in range(4)]
+    mv = tt(T.M2[:, :], T.PW[:, 48:96], T.MK[:, :], A.mult, deps=qv + [mk])
+    lsz = [ts(T.LSZ[:, 4 * k:4 * k + 4], T.NP[:, :], T.SHF[:, p:p + 1], A.add, deps=c_n + [shf]) for k, p in enumerate(dest)]
+    join(*lsz)
+    vv = as_list(T.VV, T.M2, mv)
+    lv = join(*[ts(T.LV[:, c::3], T.T16[:, 0:8:4], T.VV[:, c:c + 1], A.add, deps=[i_t] + vv) for c in range(3)])
+    ley = join(*[ts(T.LEY[:, c::3], T.P24[:, :], T.VV[:, c:c + 1], A.add, deps=vv + c_n) for c in range(3)])
+    p3 = tt(T.P3[:, :], T.WT[:, 0:48].indirect(T.LV[:, :]), T.MW[:, :], A.mult, deps=lv + mw + [wt1])
+    qk = added(96, T.P3, [p3])
+    mk3 = tt(T.M3[:, :], T.PW[:, 96:144], T.MK[:, :], A.mult, deps=qk + [mk])
+    ev = as_list(T.EV, T.M3, mk3)
+    le = join(*[ts(T.LE[:, c::3], T.T16[:, :], T.EV[:, c:c + 1], A.add, deps=[i_t] + ev) for c in range(3)])
+    arm = join(*[ac(T.ARM[:, 192 * k:192 * k + 192], T.AT[:, :].indirect(T.NBU[:, :]), deps=i_a + [nbu] + c_m,
+                    scale=[None, None, T.LO[:, :], T.HI[:, :]][k]) for k in range(4)])
     own0 = ac(T.W0[:, 0:OWNW], T.X[:, :].indirect(T.OWN[:, :]), deps=ow + [d_x])
-
-    def level(lst, ldeps, tmp, out):
-        m = tt(tmp[:, :], T.REL[:, :].indirect(lst[:, 0:3]), T.MK[:, :], A.mult, deps=rel + [mk] + ldeps)
-        return [op("v", lambda c=c: v.tensor_reduce(out[:, c:c + 1], tmp[:, 16 * c:16 * c + 16], AxisListType.X, A.add), [m])
-                for c in range(3)]
-
-    idc = ts(T.ID24[:, :], T.REL[:, 0:1], 24, A.mult, deps=rel)
-    l1 = ts(T.L1[:, 0:3], T.PO[:, 0:3], T.ID24[:, :], A.add, deps=[idc, d_po])
-    wv = level(T.L1, [l1], T.M1, T.WV)
-    l2 = [ts(T.L2[:, c:c + 1], T.WV[:, c:c + 1], 24, A.mult, T.ACF[:, c:c + 1], A.add, deps=wv + [acf]) for c in range(3)]
-    vv = level(T.L2, l2, T.M2, T.VV)
-    l3 = [ts(T.L3[:, c:c + 1], T.WV[:, c:c + 1], 24, A.mult, T.VV[:, c:c + 1], A.add, deps=wv + vv) for c in range(3)]
-    ev = level(T.L3, l3, T.M3, T.EV)
-    le = [ts(T.LE[:, c::3], T.T16[:, :], T.EV[:, c:c + 1], A.add, deps=[i_t] + ev) for c in range(3)]
-    zz = tt(T.ZZ[:, :], T.WT[:, :].indirect(T.LE[:, :]), T.ARM[:, :], A.add, deps=le + arm)
-    zs1 = ac(T.ZS1[:, :], T.ZZ[:, 0:384].indirect(T.LSZ[:, :]), deps=[zz] + lsz)
+    zz = tt(T.ZZ[:, :], T.WT[:, :].indirect(T.LE[:, :]), T.ARM[:, :], A.add, deps=le + arm + [wt2])
+    arx = join(ac(T.ARX[:, 0::2], T.ARM[:, 384:576:2], deps=arm), ac(T.ARX[:, 1::2], T.ARM[:, 577:768:2], deps=arm))
     zs2 = ac(T.ZS2[:, :], T.ZZ[:, 384:768].indirect(T.LSZ[:, :]), deps=[zz] + lsz)
-    arx = [ac(T.ARX[:, 0::2], T.ARM[:, 384:576:2], deps=[arm[2]]), ac(T.ARX[:, 1::2], T.ARM[:, 577:768:2], deps=[arm[3]])]
-    kc = tt(T.KC[:, :], T.ZZ[:, 384:576:2], T.ZZ[:, 577:768:2], A.add, deps=[zz])
-    lc = [cp(T.LC[:, 0::3], T.ZZ[:, 0:192:2], deps=[zz]), cp(T.LC[:, 2::3], T.ZZ[:, 193:384:2], deps=[zz]),
-          cp(T.LC[:, 1::3], T.KC[:, :], deps=[kc])]
-    lb = [cp(T.LB[:, 0::3], T.ZS1[:, 0::2], deps=[zs1]), cp(T.LB[:, 2::3], T.ZS1[:, 1::2], deps=[zs1])]
-    kb = tt(T.KB[:, :], T.ZS2[:, 0::2], T.ZS2[:, 1::2], A.add, deps=[zs2])
-    lb.append(cp(T.LB[:, 1::3], T.KB[:, :], deps=[kb]))
-    ley = [ts(T.LEY[:, c::3], T.P24[:, :], T.VV[:, c:c + 1], A.add, deps=vv + [p24]) for c in range(3)]
+    zs1 = ac(T.ZS1[:, :], T.ZZ[:, 0:384].indirect(T.LSZ[:, :]), deps=[zz] + lsz)
     zy1 = tt(T.ZY1[:, :], T.WT[:, 0:48].indirect(T.LEY[:, :]), T.ARM[:, 0:192], A.add, deps=ley + arm)
     zy2 = tt(T.ZY2[:, :], T.WT[:, 48:96].indirect(T.LEY[:, :]), T.ARX[:, :], A.add, deps=ley + arx)
-    ly = [cp(T.LY[:, 0::3], T.ZY1[:, 0::2], deps=[zy1]), cp(T.LY[:, 2::3], T.ZY1[:, 1::2], deps=[zy1])]
+    kb = tt(T.KB[:, :], T.ZS2[:, 0::2], T.ZS2[:, 1::2], A.add, deps=[zs2])
+    lb = [cp(T.LB[:, 0::3], T.ZS1[:, 0::2], deps=[zs1]), cp(T.LB[:, 2::3], T.ZS1[:, 1::2], deps=[zs1]),
+          cp(T.LB[:, 1::3], T.KB[:, :], deps=[kb])]
+    join(*lb)
+    kc = tt(T.KC[:, :], T.ZZ[:, 384:576:2], T.ZZ[:, 577:768:2], A.add, deps=[zz])
     ky = tt(T.KY[:, :], T.ZY2[:, 0::2], T.ZY2[:, 1::2], A.add, deps=[zy2])
-    ly.append(cp(T.LY[:, 1::3], T.KY[:, :], deps=[ky]))
+    lc = join(cp(T.LC[:, 0::3], T.ZZ[:, 0:192:2], deps=[zz]), cp(T.LC[:, 2::3], T.ZZ[:, 193:384:2], deps=[zz]),
+              cp(T.LC[:, 1::3], T.KC[:, :], deps=[kc]))
+    ly = join(cp(T.LY[:, 0::3], T.ZY1[:, 0::2], deps=[zy1]), cp(T.LY[:, 2::3], T.ZY1[:, 1::2], deps=[zy1]),
+              cp(T.LY[:, 1::3], T.KY[:, :], deps=[ky]))
 
     for k, p in enumerate(dest):
         src = [T.W0[:, :].indirect(T.LB[:, 96 * k + 24 * n:96 * k + 24 * n + 24]) for n in range(4)]
         f0, f1, f2, f3 = [T[x][:, SLW * k:SLW * k + SLW] for x in ("F0", "F1", "F2", "F3")]
         deps = lb + [own0] + arr0
-        x2 = ac(f2, src[2], deps)
-        x3 = ac(f3, src[3], deps)
-        if k == 0:
-            x0 = cp(f0, src[0], deps)
-            x1 = tt(f1, src[1], f0, A.max, deps + [x0])
-            parts, last = [f1, f2, f3], [x1, x2, x3]
-        else:
-            x0 = tt(f0, src[0], f2, A.max, deps + [x2])
-            x1 = tt(f1, src[1], f0, A.max, deps + [x0])
-            parts, last = [f1, f3], [x1, x3]
+        x0 = cp(f0, src[0], deps)
+        x1 = tt(f1, src[1], f0, A.max, deps + [x0])
+        x = join(x1, ac(f2, src[2], deps), ac(f3, src[3], deps))
         es = feng if p in far else neng
-        send([transfer(p, parts, T.W1, es, "arr1_%d" % r, 2)], last)
+        send([transfer(p, [f1, f2, f3], T.W1, es, "arr1_%d" % r, 2)], x)
         left[0] += len(es)
     arr1 = [("sem", "arr1_%d" % q, len(feng) if q in far else len(neng)) for q in others]
 
     pc = [T.PC0, T.PC1, T.PC2]
-    last_merge = [None, None, None]
-    nch, spare = [0], [0]
+    merged = [[], [], []]
+    spare = [0]
 
-    def piece(win, lists, width, out, deps, first):
-        b = nch[0] % 3
-        nch[0] += 1
-        c = spare[0]
-        spare[0] += width
-        P = pc[b][:, 0:width]
-        G2, G3, H1, H2 = [T[x][:, c:c + width] for x in ("G2", "G3", "H1", "H2")]
-        src = [win[:, :].indirect(x) for x in lists]
-        free = [last_merge[b]] if last_merge[b] is not None else []
-        if first:
+    def pieces(win, jobs, deps, stored):
+        begin, second, end = [], [], []
+        for k, (lists, width, out) in enumerate(jobs):
+            c = spare[0]
+            spare[0] += width
+            P = pc[k][:, 0:width]
+            G2, G3, H0, H1, H2 = [T[x][:, c:c + width] for x in ("G2", "G3", "H0", "H1", "H2")]
+            src = [win[:, :].indirect(x) for x in lists]
+            g2 = [ac(G2, src[2], deps)] if k else []
             g3 = ac(G3, src[3], deps)
-            p3 = ac(P, G3, [g3] + free)
-            h0 = cp(T.H0[:, 0:width], src[0], deps)
-            h1 = tt(H1, src[1], T.H0[:, 0:width], A.max, deps + [h0])
-            h2 = tt(H2, src[2], H1, A.max, deps + [h1])
-        else:
-            g2 = ac(G2, src[2], deps)
-            g3 = ac(G3, src[3], deps)
-            p3 = ac(P, G3, [g3] + free)
-            h1 = tt(H1, src[0], G2, A.max, deps + [g2])
-            h2 = tt(H2, src[1], H1, A.max, deps + [h1])
-        res = tt(out, H2, P, A.max, [h2, p3])
-        last_merge[b] = res
+            p3 = ac(P, G3, [g3] + merged[k])
+            begin.append((H1, src[0], G2, src[1], H0, g2))
+            second.append((H2, src[1 if k else 2], H1))
+            end.append((out, H2, P, p3))
+        res, h1, h2 = [], [], []
+        for k in range(len(jobs) + 1):
+            if k < len(jobs):
+                H1, s0, G2, s1, H0, g2 = begin[k]
+                if k:
+                    h1.append(tt(H1, s0, G2, A.max, deps + g2))
+                else:
+                    h0 = cp(H0, s0, deps)
+                    h1.append(tt(H1, s1, H0, A.max, deps + [h0]))
+            if k:
+                out, H2, P, p3 = end[k - 1]
+                m = tt(out, H2, P, A.max, [h2[k - 1], p3])
+                merged[k - 1] = [m]
+                res.append(m)
+                if stored:
+                    stored(k - 1, m)
+            if k < len(jobs):
+                H2, s1, H1 = second[k]
+                h2.append(tt(H2, s1, H1, A.max, deps + [h1[k]]))
         return res
 
-    own1 = []
-    for k in range(3):
-        own1.append(piece(T.W0, [T.LC[:, 72 * n + 24 * k:72 * n + 24 * k + 24] for n in range(4)], SLW,
-                          T.W1[:, SLW * k:SLW * k + SLW], lc + [own0] + arr0, False))
+    own1 = pieces(T.W0, [([T.LC[:, 72 * n + 24 * k:72 * n + 24 * k + 24] for n in range(4)], SLW, T.W1[:, SLW * k:SLW * k + SLW])
+                         for k in range(3)], lc + [own0] + arr0, None)
 
-    stores, a = [], 0
-    for k, nodes in enumerate((16, 20, 12)):
+    jobs, stores, at = [], [], [0]
+    for nodes in (16, 20, 12):
+        a = at[-1]
         c0, cw = a // 2 * 3, nodes // 2 * 3
-        x = piece(T.W1, [T.LY[:, 72 * n + c0:72 * n + c0 + cw] for n in range(4)], nodes * 24,
-                  T.YB[:, a * 24:(a + nodes) * 24], ly + own1 + arr1, k == 0)
-        stores.append(ld("y", T.y[:, a * 24:(a + nodes) * 24], T.YB[:, a * 24:(a + nodes) * 24], [x]))
-        a += nodes
+        jobs.append(([T.LY[:, 72 * n + c0:72 * n + c0 + cw] for n in range(4)], nodes * 24, T.YB[:, a * 24:(a + nodes) * 24]))
+        at.append(a + nodes)
+
+    def store(k, m):
+        a, b = at[k] * 24, at[k + 1] * 24
+        stores.append(ld("y", T.y[:, a:b], T.YB[:, a:b], [m]))
+
+    pieces(T.W1, jobs, ly + own1 + arr1, store)
     op("y", None, stores, "w")
     op("g", None, [("sem", "left", left[0])], "w")
 
-    users = [[] for _ in ops]
+    used, total = set(), {}
     for o in ops:
-        for d in o["deps"]:
-            if not isinstance(d, tuple):
-                users[d].append(o["q"])
-    names, made, total, gname = {}, [0], {}, {}
-    for k, o in enumerate(ops):
-        if o["grp"]:
-            total[o["grp"]] = total.get(o["grp"], 0) + (16 if o["kind"] == "d" else 1)
-    for k, o in enumerate(ops):
-        if o["kind"] in "cd" and users[k]:
-            if o["kind"] == "c" and all(q == o["q"] for q in users[k]):
-                names[k] = ("self_" + o["q"], 0, 0)
-                continue
-            inc = 16 if o["kind"] == "d" else 1
-            name = gname.get(o["grp"])
-            if name is None:
-                name = "x%d" % made[0]
-                made[0] += 1
-                if o["grp"]:
-                    gname[o["grp"]] = name
-            names[k] = (name, inc, total.get(o["grp"], inc))
+        used.update(ops[d]["grp"] for d in o["deps"] if not isinstance(d, tuple))
+    for o in ops:
+        total[o["grp"]] = total.get(o["grp"], 0) + (16 if o["kind"] == "d" else 1)
+    names = {k: "x%d" % n for n, k in enumerate(sorted(used))}
     done = {q: {} for q in queues}
-    count = {q: 0 for q in queues}
 
     def wait(q, name, val):
         if done[q].get(name, 0) < val:
             queues[q].wait_ge(T.sem[name], val)
             done[q][name] = val
 
-    for k, o in enumerate(ops):
-        q = o["q"]
+    for o in ops:
         for d in o["deps"]:
             if isinstance(d, tuple):
-                wait(q, d[1], d[2])
-            elif names[d][1] == 0:
-                wait(q, names[d][0], count[q])
+                wait(o["q"], d[1], d[2])
             else:
-                wait(q, names[d][0], names[d][2])
-        if o["kind"] == "w":
-            continue
-        ins = o["f"]()
-        if k in names:
-            if names[k][1] == 0:
-                count[q] += 1
-                ins.then_inc(T.sem[names[k][0]], 1)
-            else:
-                ins.then_inc(T.sem[names[k][0]], names[k][2] if False else names[k][1])
-    for q in queues:
-        if count[q]:
-            wait(q, "self_" + q, count[q])
+                k = ops[d]["grp"]
+                wait(o["q"], names[k], total[k])
+        if o["kind"] != "w":
+            ins = o["f"]()
+            if o["grp"] in names:
+                ins.then_inc(T.sem[names[o["grp"]]], 16 if o["kind"] == "d" else 1)

@@ -1,48 +1,49 @@
 from concourse.bass import DstId, RemoteDMATransfer
 from concourse.mybir import AluOpType, AxisListType, ActivationFunctionType
 
-NX = 130
+NX = 140
 SCRATCH = {
     "X": ("sbuf", [128, 1152], "float32"), "TR": ("sbuf", [128, 48], "int32"), "PO": ("sbuf", [128, 4], "int32"),
     "SHN": ("sbuf", [128, 4], "int32"), "NB": ("sbuf", [128, 12], "int32"), "AC": ("sbuf", [128, 4], "int32"),
+    "CT": ("sbuf", [128, 48], "int32"),
     "IP": ("sbuf", [128, 2], "int32"), "DD": ("sbuf", [128, 128], "float32"), "GI": ("sbuf", [128, 128], "float32"),
-    "IM": ("sbuf", [128, 48], "int32"), "IM2": ("sbuf", [128, 48], "int32"),
-    "CI": ("sbuf", [128, 192], "float32"), "C48": ("sbuf", [128, 96], "float32"), "T16": ("sbuf", [128, 16], "float32"),
-    "N4": ("sbuf", [128, 4], "float32"), "AT": ("sbuf", [128, 112], "float32"),
+    "IM": ("sbuf", [128, 16], "int32"), "IM2": ("sbuf", [128, 16], "int32"), "MK": ("sbuf", [128, 16], "float32"),
+    "C48": ("sbuf", [128, 96], "float32"), "S4": ("sbuf", [128, 4], "float32"),
+    "SQ4": ("sbuf", [128, 4], "float32"), "N4": ("sbuf", [128, 4], "float32"), "NP": ("sbuf", [128, 4], "float32"),
+    "NM": ("sbuf", [128, 4], "float32"), "AT": ("sbuf", [128, 112], "float32"), "I24": ("sbuf", [128, 24], "float32"),
     "B1": ("sbuf", [128, 2], "int32"), "B8": ("sbuf", [128, 2], "int32"), "BQ": ("sbuf", [128, 2], "int32"),
-    "BG": ("sbuf", [128, 2], "int32"), "PG": ("sbuf", [128, 1], "float32"), "U2": ("sbuf", [128, 2], "float32"),
-    "LO": ("sbuf", [128, 1], "float32"),
-    "HI": ("sbuf", [128, 1], "float32"), "P48": ("sbuf", [128, 1], "float32"), "P192": ("sbuf", [128, 1], "float32"),
-    "P24C": ("sbuf", [128, 1], "float32"), "P24": ("sbuf", [128, 4], "float32"),
-    "SH": ("sbuf", [128, 128], "bfloat16"), "SL": ("sbuf", [128, 128], "bfloat16"), "ON": ("sbuf", [128, 128], "bfloat16"),
-    "MK": ("sbuf", [128, 48], "float32"), "NP": ("sbuf", [128, 4], "float32"),
-    "TRB": ("sbuf", [128, 48], "bfloat16"), "WT": ("sbuf", [128, 96], "float32"), "LP": ("sbuf", [128, 12], "uint16"),
-    "NN": ("sbuf", [128, 192], "float32"), "LSH": ("sbuf", [128, 4], "uint16"), "SHF": ("sbuf", [128, 4], "float32"),
-    "R1": ("sbuf", [128, 48], "float32"), "R2": ("sbuf", [128, 48], "float32"), "K1": ("sbuf", [128, 24], "float32"),
-    "LA": ("sbuf", [128, 72], "uint16"), "KO": ("sbuf", [128, 24], "float32"), "OWN": ("sbuf", [128, 72], "uint16"),
+    "BG": ("sbuf", [128, 2], "int32"), "PG": ("sbuf", [128, 1], "float32"), "QF": ("sbuf", [128, 2], "float32"),
+    "LO": ("sbuf", [128, 1], "float32"), "HI": ("sbuf", [128, 1], "float32"), "PQ": ("sbuf", [128, 2], "float32"),
+    "PQ4": ("sbuf", [128, 2], "float32"),
+    "SH": ("sbuf", [128, 128], "float16"), "SL": ("sbuf", [128, 128], "float16"), "ON": ("sbuf", [128, 128], "bfloat16"),
+    "SHW": ("sbuf", [128, 128], "float32"), "SLW": ("sbuf", [128, 128], "float32"), "ID": ("sbuf", [128, 128], "float32"),
+    "RN": ("sbuf", [128, 256], "bfloat16"), "BL": ("sbuf", [128, 32], "uint16"),
+    "WT": ("sbuf", [128, 48], "float32"), "LP": ("sbuf", [128, 6], "uint16"),
+    "NN": ("sbuf", [128, 96], "float32"), "LSH": ("sbuf", [128, 6], "uint16"), "SHF": ("sbuf", [128, 4], "float32"),
+    "RR": ("sbuf", [128, 96], "float16"),
+    "LA": ("sbuf", [128, 72], "uint16"), "OWN": ("sbuf", [128, 72], "uint16"),
     "NBU": ("sbuf", [128, 12], "uint16"), "IT": ("sbuf", [128, 16], "float32"), "IDC": ("sbuf", [128, 1], "float32"),
-    "EQ": ("sbuf", [128, 2], "float32"), "MW": ("sbuf", [128, 96], "float32"),
-    "LM": ("sbuf", [128, 6], "uint16"), "LV": ("sbuf", [128, 6], "uint16"),
-    "P1": ("sbuf", [128, 96], "bfloat16"), "P2": ("sbuf", [128, 96], "bfloat16"), "P3": ("sbuf", [128, 96], "bfloat16"),
-    "M2": ("sbuf", [128, 48], "float32"), "M3": ("sbuf", [128, 48], "float32"),
-    "VV": ("sbuf", [128, 4], "float32"), "EV": ("sbuf", [128, 4], "float32"),
-    "LE": ("sbuf", [128, 48], "uint16"), "ARM": ("sbuf", [128, 768], "float32"), "ARX": ("sbuf", [128, 192], "float32"),
-    "ZZ": ("sbuf", [128, 768], "float32"), "LSZ": ("sbuf", [128, 12], "uint16"),
-    "ZS1": ("sbuf", [128, 192], "float32"), "ZS2": ("sbuf", [128, 192], "float32"), "KB": ("sbuf", [128, 96], "float32"),
-    "LB": ("sbuf", [128, 288], "uint16"), "KC": ("sbuf", [128, 96], "float32"), "LC": ("sbuf", [128, 288], "uint16"),
-    "LEY": ("sbuf", [128, 12], "uint16"), "ZY1": ("sbuf", [128, 192], "float32"), "ZY2": ("sbuf", [128, 192], "float32"),
-    "KY": ("sbuf", [128, 96], "float32"), "LY": ("sbuf", [128, 288], "uint16"),
+    "LM": ("sbuf", [128, 6], "uint16"), "CW": ("sbuf", [128, 64], "float32"), "BD": ("sbuf", [128, 512], "bfloat16"),
+    "TRG": ("sbuf", [128, 96], "float32"), "MS": ("sbuf", [128, 96], "float32"),
+    "OA": ("sbuf", [128, 96], "bfloat16"), "OV": ("sbuf", [128, 96], "bfloat16"), "OK": ("sbuf", [128, 96], "bfloat16"),
+    "ARM": ("sbuf", [128, 192], "float32"), "Z": ("sbuf", [128, 384], "float32"), "ZY": ("sbuf", [128, 384], "float32"),
+    "LS1": ("sbuf", [128, 12], "uint16"), "LS2": ("sbuf", [128, 12], "uint16"),
+    "ZS1": ("sbuf", [128, 192], "float32"), "ZS2": ("sbuf", [128, 192], "float16"),
+    "LB": ("sbuf", [128, 288], "uint16"), "LC": ("sbuf", [128, 288], "uint16"), "LY": ("sbuf", [128, 288], "uint16"),
     "W0": ("sbuf", [128, 2304], "float32"), "W1": ("sbuf", [128, 2304], "float32"),
     "SA": ("sbuf", [128, 1152], "float32"), "YB": ("sbuf", [128, 1152], "float32"),
     "F0": ("sbuf", [128, 1152], "float32"), "F1": ("sbuf", [128, 1152], "float32"),
     "F2": ("sbuf", [128, 1152], "float32"), "F3": ("sbuf", [128, 1152], "float32"),
     "G2": ("sbuf", [128, 2304], "float32"), "G3": ("sbuf", [128, 2304], "float32"),
     "H0": ("sbuf", [128, 2304], "float32"), "H1": ("sbuf", [128, 2304], "float32"), "H2": ("sbuf", [128, 2304], "float32"),
-    "PT": ("psum", [128, 512], "float32"), "PW": ("psum", [128, 512], "float32"),
+    "PT": ("psum", [128, 512], "float32"), "PY": ("psum", [128, 512], "float32"), "PV": ("psum", [128, 512], "float32"),
+    "PK": ("psum", [128, 512], "float32"), "PM": ("psum", [128, 512], "float32"),
     "PC0": ("psum", [128, 512], "float32"), "PC1": ("psum", [128, 512], "float32"), "PC2": ("psum", [128, 512], "float32"),
 }
 SEMAPHORES = ["left"] + ["arr%d_%d" % (t, q) for t in range(2) for q in range(4)] + ["x%d" % k for k in range(NX)]
 OWNW, SLW = 48 * 24, 16 * 24
+JOBS0 = [8, 12, 12, 16]
+JOBS1 = [8, 12, 16, 12]
 
 
 def place(q, p):
@@ -79,10 +80,8 @@ def rank_program(g, core, T, topo):
     def cp(out, a, deps=()):
         return op("v", lambda: v.tensor_copy(out, a), deps)
 
-    def ac(out, a, deps=(), scale=None):
-        if scale is None:
-            return op("s", lambda: s.activation(out, a, ACT.Copy), deps)
-        return op("s", lambda: s.activation(out, a, ACT.Identity, scale=scale), deps)
+    def ac(out, a, deps=()):
+        return op("s", lambda: s.activation(out, a, ACT.Copy), deps)
 
     def mm(out, lhs, rhs, start, stop, deps):
         return op("t", lambda: t.matmul(out, lhs, rhs, start, stop), deps)
@@ -106,8 +105,9 @@ def rank_program(g, core, T, topo):
     d_rd = ld("y", T.TR[:, 24:48], T.rel[:, 192:576])
     d_sh = ld("s", T.SHN[:, 0:4], T.shown[:, :])
     d_x = ld("s", T.X[:, :], T.x[:, :])
-    d_ac = ld("y", T.AC[:, 0:3], T.act[:, :])
-    d_nb = ld("y", T.NB[:, 0:12], T.nbr[:, :])
+    d_ac = ld("s", T.AC[:, 0:3], T.act[:, :])
+    d_nb = ld("s", T.NB[:, 0:12], T.nbr[:, :])
+    d_ct = join(ld("s", T.CT[:, 0:24], T.ct[:, 0:384]), ld("s", T.CT[:, 24:48], T.ct[:, 192:576]))
     join(d_ra, d_rd)
 
     def iota(out, pat, base, cm, f32=True):
@@ -118,10 +118,11 @@ def rank_program(g, core, T, topo):
     i_p = iota(T.IP[:, :], [[0, 2]], 0, 1, False)
     i_d = iota(T.DD[:, :], [[1, 128]], 0, -1)
     i_c = iota(T.C48[:, :], [[0, 2], [24, 48]], 0, 0)
-    i_m = iota(T.IM[:, :], [[0, 3], [1, 16]], 0, -1, False)
-    i_n = iota(T.N4[:, :], [[48, 4]], 0, 0)
+    i_m = iota(T.IM[:, :], [[1, 16]], 0, -1, False)
     i_g = iota(T.GI[:, :], [[1, 8], [0, 16]], 0, 0)
-    i_t = iota(T.T16[:, :], [[24, 4], [0, 4]], 0, 0)
+    i_4 = iota(T.S4[:, :], [[24, 2], [8, 2]], -48, 0)
+    i_24 = iota(T.I24[:, :], [[1, 24]], 0, 0)
+    i_n = iota(T.N4[:, :], [[48, 4]], 0, 0)
     hole = 48 + 16 * r + 16
     i_a = [iota(T.AT[:, 0:hole], [[24, hole]], 0, 0)]
     if hole < 112:
@@ -134,51 +135,43 @@ def rank_program(g, core, T, topo):
                ts(T.BG[:, :], T.IP[:, :], 4, A.arith_shift_right, deps=[i_p]))
     c_m = join(ts(T.LO[:, :], T.B8[:, 0:1], 0, A.is_equal, deps=c_b),
                ts(T.HI[:, :], T.B8[:, 0:1], 0, A.is_gt, deps=c_b),
-               ts(T.P48[:, :], T.B1[:, 0:1], 48, A.mult, deps=c_b),
-               ts(T.P192[:, :], T.B1[:, 0:1], 192, A.mult, deps=c_b),
-               ts(T.P24C[:, :], T.B1[:, 0:1], 24, A.mult, deps=c_b),
+               ts(T.PQ[:, 0:1], T.B1[:, 0:1], 48, A.mult, deps=c_b),
+               ts(T.PQ[:, 1:2], T.B1[:, 0:1], -48, A.mult, 48, A.add, deps=c_b),
                cp(T.PG[:, :], T.BG[:, 0:1], deps=c_b),
-               ts(T.U2[:, 0:1], T.BQ[:, 0:1], 1, A.add, deps=c_b))
+               cp(T.QF[:, 0:1], T.BQ[:, 0:1], deps=c_b))
     c_s = join(ts(T.SH[:, :], T.DD[:, :], -8, A.is_equal, T.HI[:, :], A.mult, deps=[i_d] + c_m),
                ts(T.SL[:, :], T.DD[:, :], 8, A.is_equal, T.LO[:, :], A.mult, deps=[i_d] + c_m))
-    c_u = ts(T.U2[:, 1:2], T.BQ[:, 0:1], 9, A.add, T.HI[:, :], A.mult, deps=c_b + c_m)
-    c_ci = join(cp(T.CI[:, 0:96], T.C48[:, :], deps=[i_c]),
-                ts(T.CI[:, 96:144], T.C48[:, 0:48], T.LO[:, :], A.mult, deps=[i_c] + c_m),
-                ts(T.CI[:, 144:192], T.C48[:, 0:48], T.HI[:, :], A.mult, deps=[i_c] + c_m))
+    c_f = join(ts(T.SHW[:, :], T.DD[:, :], -8, A.is_equal, T.HI[:, :], A.mult, deps=[i_d] + c_m),
+               ts(T.SLW[:, :], T.DD[:, :], 8, A.is_equal, T.LO[:, :], A.mult, deps=[i_d] + c_m))
     im2 = ts(T.IM2[:, :], T.IM[:, :], 15, A.bitwise_and, deps=[i_m])
-    c_n = join(ts(T.NP[:, :], T.N4[:, :], T.P192[:, :], A.add, deps=[i_n] + c_m),
-               ts(T.P24[:, :], T.N4[:, :], 0, A.mult, T.P24C[:, :], A.add, deps=[i_n] + c_m))
+    zc = op("v", lambda: v.memset(T.CW[:, 48:64], 0.0))
     mk = ts(T.MK[:, :], T.IM2[:, :], 0, A.is_equal, deps=[im2])
+    c_q = ts(T.QF[:, 1:2], T.QF[:, 0:1], 8, A.add, T.HI[:, :], A.mult, deps=c_m)
     on = ts(T.ON[:, :], T.GI[:, :], T.PG[:, :], A.is_equal, deps=[i_g] + c_m)
+    sq4 = ts(T.SQ4[:, :], T.S4[:, :], T.QF[:, 0:1], A.add, deps=[i_4] + c_m)
 
-    trb = cp(T.TRB[:, :], T.TR[:, :], deps=[d_ra, d_rd])
-    m1 = mm(T.PT[:, 0:24], T.SH[:, :], T.TRB[:, 24:48], True, True, [trb] + c_s)
-    m2 = mm(T.PT[:, 24:48], T.SL[:, :], T.TRB[:, 0:24], True, True, [trb] + c_s)
-    join(m1, m2)
-    wt1 = cp(T.WT[:, 0:48], T.TR[:, :], deps=[d_ra, d_rd])
-    lp = join(*[ts(T.LP[:, 3 * k:3 * k + 3], T.PO[:, 0:3], 24 * k, A.add, deps=[d_po]) for k in range(4)])
-    wt2 = cp(T.WT[:, 48:96], T.PT[:, 0:48], deps=[m1, m2])
-    lsh = join(*[ts(T.LSH[:, k:k + 1], T.SHN[:, p:p + 1], T.P48[:, :], A.add, deps=[d_sh] + c_m) for k, p in enumerate(dest)])
-    nn = tt(T.NN[:, :], T.WT[:, :].indirect(T.LP[:, 0:12]), T.CI[:, :], A.add, deps=lp + [wt1, wt2] + c_ci)
-    idt = tt(T.IT[:, :], T.WT[:, 0:16], T.MK[:, 0:16], A.mult, deps=[wt1, mk])
-    r1 = cp(T.R1[:, :], T.NN[:, 0:96].indirect(T.LSH[:, 0:3]), deps=[nn] + lsh)
-    r2 = ac(T.R2[:, :], T.NN[:, 96:192].indirect(T.LSH[:, 0:3]), deps=[nn] + lsh)
+    lp = join(*[ts(T.LP[:, 3 * k:3 * k + 3], T.PO[:, 0:3], 24 * k, A.add, deps=[d_po]) for k in range(2)])
+    nn = tt(T.NN[:, :], T.TR[:, :].indirect(T.LP[:, 0:6]), T.C48[:, :], A.add, deps=lp + [d_ra, d_rd, i_c])
+    shf = cp(T.SHF[:, :], T.SHN[:, :], deps=[d_sh])
+    wt = cp(T.WT[:, :], T.TR[:, :], deps=[d_ra, d_rd])
+    lsh = join(*[ts(T.LSH[:, k::3], T.PQ[:, :], T.SHF[:, p:p + 1], A.add, deps=c_m + [shf]) for k, p in enumerate(dest)])
+    rr = cp(T.RR[:, :], T.NN[:, :].indirect(T.LSH[:, 0:6]), deps=[nn] + lsh)
+    trg = ac(T.TRG[:, :], T.WT[:, :].indirect(T.LP[:, 0:6]), deps=lp + [wt])
+    idt = tt(T.IT[:, :], T.WT[:, 0:16], T.MK[:, :], A.mult, deps=[wt, mk])
+    la = [cp(T.LA[:, 0::3], T.RR[:, 0:48:2], deps=[rr]), cp(T.LA[:, 2::3], T.RR[:, 1:48:2], deps=[rr])]
+    qa = join(mm(T.PT[:, 0:24], T.SH[:, :], T.RR[:, 48:96:2], True, False, [rr] + c_s),
+              mm(T.PT[:, 0:24], T.SL[:, :], T.RR[:, 49:96:2], False, True, [rr] + c_s))
     idc = op("v", lambda: v.tensor_reduce(T.IDC[:, :], T.IT[:, :], AxisListType.X, A.add), [idt])
-    la = [cp(T.LA[:, 0::3], T.R1[:, 0::2], deps=[r1]), cp(T.LA[:, 2::3], T.R1[:, 1::2], deps=[r1])]
-    k1 = tt(T.K1[:, :], T.R2[:, 0::2], T.R2[:, 1::2], A.add, deps=[r2])
-    eq = ts(T.EQ[:, :], T.U2[:, :], T.IDC[:, :], A.subtract, 1, A.is_equal, deps=[idc, c_u] + c_m)
-    la.append(cp(T.LA[:, 1::3], T.K1[:, :], deps=[k1]))
+    qo = join(mm(T.PM[:, 0:24], T.SHW[:, :], T.NN[:, 48:96:2], True, False, [nn] + c_f),
+              mm(T.PM[:, 0:24], T.SLW[:, :], T.NN[:, 1:48:2], False, True, [nn] + c_f))
+    ow = [cp(T.OWN[:, 0::3], T.NN[:, 0:48:2], deps=[nn])]
+    la.append(cp(T.LA[:, 1::3], T.PT[:, 0:24], deps=qa))
     join(*la)
-    p1 = join(*[ts(T.P1[:, 48 * k:48 * k + 48], T.WT[:, 24 * k:24 * k + 24].indirect(T.LP[:, 0:3]), T.EQ[:, k:k + 1], A.mult,
-                   deps=lp + [wt1, eq]) for k in range(2)])
 
-    sa = []
-    for k in range(3):
-        a, b = SLW * k, SLW * k + SLW // 2
-        sa.append([cp(T.SA[:, a:b], T.X[:, :].indirect(T.LA[:, 24 * k:24 * k + 12]), deps=la + [d_x]),
-                   ac(T.SA[:, b:a + SLW], T.X[:, :].indirect(T.LA[:, 24 * k + 12:24 * k + 24]), deps=la + [d_x])])
-    join(*(sa[0] + sa[1]))
-    join(*sa[2])
+    bl = join(*[ts(T.BL[:, 8 * k:8 * k + 8], T.ON[:, 0::16], T.SQ4[:, k:k + 1], A.mult, 48, A.add, deps=[on, sq4]) for k in range(4)])
+    ow.append(cp(T.OWN[:, 2::3], T.NN[:, 49:96:2], deps=[nn]))
+    ow.append(cp(T.OWN[:, 1::3], T.PM[:, 0:24], deps=qo))
+    join(*ow)
 
     def transfer(p, srcs, win, es, arr, alu=0):
         rid, pid = topo.addr(T.cores[p], core)
@@ -186,132 +179,160 @@ def rank_program(g, core, T, topo):
         return RemoteDMATransfer(srcs=srcs, dsts=[win[:, c:c + SLW]], dst_ids=[DstId(rid=rid, pnc=pid)],
                                  dma_engine_mask=bits(es), remote_sem=T.sem[arr], alu_op=alu)
 
-    def send(transfers, deps):
-        return op("g", lambda: g.remote_dma_fused(transfers, local_sem=T.sem["left"]), deps, "r")
+    left = [0]
 
-    half = [feng[:len(feng) // 2], feng[len(feng) // 2:]]
-    send([transfer(p, [T.SA[:, SLW * k:SLW * k + SLW]], T.W0, half[k], "arr0_%d" % r) for k, p in enumerate(far)], sa[0] + sa[1])
-    send([transfer(near[0], [T.SA[:, 2 * SLW:3 * SLW]], T.W0, neng, "arr0_%d" % r)], sa[2])
-    left = [len(feng) + len(neng)]
-    arr0 = [("sem", "arr0_%d" % q, len(half[0]) if q in far else len(neng)) for q in others]
-
-    def added(c, part, deps):
-        return join(mm(T.PW[:, c:c + 48], T.ON[:, :], part[:, 0:48], True, False, deps + [on]),
-                    mm(T.PW[:, c:c + 48], T.ON[:, :], part[:, 48:96], False, True, deps + [on]))
-
-    def as_list(out, tmp, m):
-        return join(*[op("v", lambda c=c: v.tensor_reduce(out[:, c:c + 1], tmp[:, 16 * c:16 * c + 16], AxisListType.X, A.add), [m])
-                      for c in range(3)])
-
-    qw = added(0, T.P1, p1)
-    nbu = cp(T.NBU[:, :], T.NB[:, :], deps=[d_nb])
-    lm = join(*[ts(T.LM[:, 3 * k:3 * k + 3], T.AC[:, 0:3], 24 * k, A.add, deps=[d_ac]) for k in range(2)])
-    mw = join(*[ts(T.MW[:, 48 * k:48 * k + 48], T.PW[:, 0:48], 1, A.add, T.U2[:, k:k + 1], A.is_equal, deps=qw + [c_u] + c_m)
-                for k in range(2)])
-    ow = [cp(T.OWN[:, 0::3], T.NN[:, 0:48:2], deps=[nn]), cp(T.OWN[:, 2::3], T.NN[:, 49:96:2], deps=[nn])]
-    ko = tt(T.KO[:, :], T.NN[:, 96:144:2], T.NN[:, 145:192:2], A.add, deps=[nn])
-    p2 = tt(T.P2[:, :], T.WT[:, 0:48].indirect(T.LM[:, :]), T.MW[:, :], A.mult, deps=lm + mw + [wt1])
-    qv = added(48, T.P2, [p2])
-    ow.append(cp(T.OWN[:, 1::3], T.KO[:, :], deps=[ko]))
-    join(*ow)
-    shf = cp(T.SHF[:, :], T.SHN[:, :], deps=[d_sh])
-    mv = tt(T.M2[:, :], T.PW[:, 48:96], T.MK[:, :], A.mult, deps=qv + [mk])
-    lsz = [ts(T.LSZ[:, 4 * k:4 * k + 4], T.NP[:, :], T.SHF[:, p:p + 1], A.add, deps=c_n + [shf]) for k, p in enumerate(dest)]
-    join(*lsz)
-    vv = as_list(T.VV, T.M2, mv)
-    lv = join(*[ts(T.LV[:, c::3], T.T16[:, 0:8:4], T.VV[:, c:c + 1], A.add, deps=[i_t] + vv) for c in range(3)])
-    ley = join(*[ts(T.LEY[:, c::3], T.P24[:, :], T.VV[:, c:c + 1], A.add, deps=vv + c_n) for c in range(3)])
-    p3 = tt(T.P3[:, :], T.WT[:, 0:48].indirect(T.LV[:, :]), T.MW[:, :], A.mult, deps=lv + mw + [wt1])
-    qk = added(96, T.P3, [p3])
-    mk3 = tt(T.M3[:, :], T.PW[:, 96:144], T.MK[:, :], A.mult, deps=qk + [mk])
-    ev = as_list(T.EV, T.M3, mk3)
-    le = join(*[ts(T.LE[:, c::3], T.T16[:, :], T.EV[:, c:c + 1], A.add, deps=[i_t] + ev) for c in range(3)])
-    arm = join(*[ac(T.ARM[:, 192 * k:192 * k + 192], T.AT[:, :].indirect(T.NBU[:, :]), deps=i_a + [nbu] + c_m,
-                    scale=[None, None, T.LO[:, :], T.HI[:, :]][k]) for k in range(4)])
-    own0 = ac(T.W0[:, 0:OWNW], T.X[:, :].indirect(T.OWN[:, :]), deps=ow + [d_x])
-    zz = tt(T.ZZ[:, :], T.WT[:, :].indirect(T.LE[:, :]), T.ARM[:, :], A.add, deps=le + arm + [wt2])
-    arx = join(ac(T.ARX[:, 0::2], T.ARM[:, 384:576:2], deps=arm), ac(T.ARX[:, 1::2], T.ARM[:, 577:768:2], deps=arm))
-    zs2 = ac(T.ZS2[:, :], T.ZZ[:, 384:768].indirect(T.LSZ[:, :]), deps=[zz] + lsz)
-    zs1 = ac(T.ZS1[:, :], T.ZZ[:, 0:384].indirect(T.LSZ[:, :]), deps=[zz] + lsz)
-    zy1 = tt(T.ZY1[:, :], T.WT[:, 0:48].indirect(T.LEY[:, :]), T.ARM[:, 0:192], A.add, deps=ley + arm)
-    zy2 = tt(T.ZY2[:, :], T.WT[:, 48:96].indirect(T.LEY[:, :]), T.ARX[:, :], A.add, deps=ley + arx)
-    kb = tt(T.KB[:, :], T.ZS2[:, 0::2], T.ZS2[:, 1::2], A.add, deps=[zs2])
-    lb = [cp(T.LB[:, 0::3], T.ZS1[:, 0::2], deps=[zs1]), cp(T.LB[:, 2::3], T.ZS1[:, 1::2], deps=[zs1]),
-          cp(T.LB[:, 1::3], T.KB[:, :], deps=[kb])]
-    join(*lb)
-    kc = tt(T.KC[:, :], T.ZZ[:, 384:576:2], T.ZZ[:, 577:768:2], A.add, deps=[zz])
-    ky = tt(T.KY[:, :], T.ZY2[:, 0::2], T.ZY2[:, 1::2], A.add, deps=[zy2])
-    lc = join(cp(T.LC[:, 0::3], T.ZZ[:, 0:192:2], deps=[zz]), cp(T.LC[:, 2::3], T.ZZ[:, 193:384:2], deps=[zz]),
-              cp(T.LC[:, 1::3], T.KC[:, :], deps=[kc]))
-    ly = join(cp(T.LY[:, 0::3], T.ZY1[:, 0::2], deps=[zy1]), cp(T.LY[:, 2::3], T.ZY1[:, 1::2], deps=[zy1]),
-              cp(T.LY[:, 1::3], T.KY[:, :], deps=[ky]))
+    def send(p, srcs, win, arr, alu, deps):
+        es = feng if p in far else neng
+        left[0] += len(es)
+        x = transfer(p, srcs, win, es, arr, alu)
+        return op("g", lambda: g.remote_dma_fused([x], local_sem=T.sem["left"]), deps, "r")
 
     for k, p in enumerate(dest):
-        src = [T.W0[:, :].indirect(T.LB[:, 96 * k + 24 * n:96 * k + 24 * n + 24]) for n in range(4)]
+        a, b = SLW * k, SLW * k + SLW // 2
+        x = join(cp(T.SA[:, a:b], T.X[:, :].indirect(T.LA[:, 24 * k:24 * k + 12]), deps=la + [d_x]),
+                 ac(T.SA[:, b:a + SLW], T.X[:, :].indirect(T.LA[:, 24 * k + 12:24 * k + 24]), deps=la + [d_x]))
+        send(p, [T.SA[:, a:a + SLW]], T.W0, "arr0_%d" % r, 0, x)
+    arr0, arr1 = [[("sem", "arr%d_%d" % (k, q), len(feng) if q in far else len(neng)) for q in others] for k in range(2)]
+
+    lm = join(*[cp(T.LM[:, 3 * k:3 * k + 3], T.AC[:, 0:3], deps=[d_ac]) for k in range(2)])
+    cw = join(cp(T.CW[:, 0:24], T.CT[:, 0:24], deps=d_ct), ts(T.CW[:, 24:48], T.CT[:, 24:48], T.HI[:, :], A.mult, deps=d_ct + c_m))
+    ms = ac(T.MS[:, :], T.I24[:, :].indirect(T.LM[:, :]), deps=lm + [i_24])
+    nbu = cp(T.NBU[:, :], T.NB[:, :], deps=[d_nb])
+    bd = join(ac(T.BD[:, 0:256], T.CW[:, :].indirect(T.BL[:, 0:16]), deps=bl + cw + [zc]),
+              cp(T.BD[:, 256:512], T.CW[:, :].indirect(T.BL[:, 16:32]), deps=bl + cw + [zc]))
+    oa = tt(T.OA[:, :], T.TRG[:, :], T.MS[:, :], A.is_equal, deps=[trg, ms])
+    arm = ac(T.ARM[:, :], T.AT[:, :].indirect(T.NBU[:, :]), deps=i_a + [nbu])
+
+    def rows(out, oh, deps):
+        return join(*[mm(out[:, 48 * h:48 * h + 48], T.BD[:, 256 * k + 128 * h:256 * k + 128 * h + 128], oh[:, 48 * k:48 * k + 48],
+                         k == 0, k == 1, deps) for h in range(2) for k in range(2)])
+
+    def plus(out, P, deps):
+        return join(*[tt(out[:, 192 * h + 48 * n:192 * h + 48 * n + 48], T.ARM[:, 48 * n:48 * n + 48], P[:, 48 * h:48 * h + 48], A.add, deps)
+                      for h in range(2) for n in range(4)])
+
+    def middle(P, up, down, even, odd, deps):
+        return join(mm(P, up, even, True, False, deps), mm(P, down, odd, False, True, deps))
+
+    qy = rows(T.PY, T.OA, [oa] + bd)
+    c_r = join(ts(T.RN[:, 0:128], T.ON[:, :], T.QF[:, 0:1], A.mult, deps=[on] + c_m),
+               ts(T.RN[:, 128:256], T.ON[:, :], T.QF[:, 1:2], A.mult, deps=[on, c_q]))
+    c_p = ts(T.PQ4[:, :], T.PQ[:, :], 4, A.mult, deps=c_m)
+    idm = ts(T.ID[:, :], T.DD[:, :], 0, A.is_equal, deps=[i_d])
+    c_np = join(ts(T.NP[:, :], T.N4[:, :], T.PQ4[:, 0:1], A.add, deps=[i_n, c_p]),
+                ts(T.NM[:, :], T.N4[:, :], T.PQ4[:, 1:2], A.add, deps=[i_n, c_p]))
+    own0 = [ac(T.W0[:, 0:OWNW], T.X[:, :].indirect(T.OWN[:, :]), deps=ow + [d_x])]
+    ov = ts(T.OV[:, :], T.PY[:, 0:96], T.IDC[:, :], A.is_equal, deps=qy + [idc])
+    qv = join(*[mm(T.PV[:, 48 * h:48 * h + 48], T.RN[:, 128 * k:128 * k + 128], T.OV[:, 48 * k:48 * k + 48], k == 0, k == 1, [ov] + c_r)
+                for h in range(2) for k in range(2)])
+    zy = plus(T.ZY, T.PY, qy + [arm])
+    ok = tt(T.OK[:, :], T.TRG[:, :], T.PV[:, 0:96], A.is_equal, deps=qv + [trg])
+    qk = rows(T.PK, T.OK, [ok] + bd)
+    ls = join(*([ts(T.LS2[:, 4 * k:4 * k + 4], T.NM[:, :], T.SHF[:, p:p + 1], A.add, deps=c_np + [shf]) for k, p in enumerate(dest)] +
+                [ts(T.LS1[:, 4 * k:4 * k + 4], T.NP[:, :], T.SHF[:, p:p + 1], A.add, deps=c_np + [shf]) for k, p in enumerate(dest)]))
+    qz = middle(T.PV[:, 0:96], T.SHW[:, :], T.SLW[:, :], T.ZY[:, 192:384:2], T.ZY[:, 1:192:2], zy + c_f + [ok])
+    ly = [cp(T.LY[:, 0::3], T.ZY[:, 0:192:2], deps=zy)]
+    z = plus(T.Z, T.PK, qk + [arm])
+    ly.append(cp(T.LY[:, 2::3], T.ZY[:, 193:384:2], deps=zy))
+    zs2 = ts(T.ZS2[:, :], T.Z[:, :].indirect(T.LS2[:, :]), -OWNW, A.add, deps=z + ls)
+    zs1 = ac(T.ZS1[:, :], T.Z[:, :].indirect(T.LS1[:, :]), deps=z + ls)
+    qb = middle(T.PM[:, 0:96], T.SH[:, :], T.SL[:, :], T.ZS2[:, 0::2], T.ZS2[:, 1::2], [zs2] + c_s + ow)
+    qc = middle(T.PT[:, 0:96], T.SHW[:, :], T.SLW[:, :], T.Z[:, 192:384:2], T.Z[:, 1:192:2], z + c_f + la)
+    ly.append(cp(T.LY[:, 1::3], T.PV[:, 0:96], deps=qz))
+    join(*ly)
+    lc = [cp(T.LC[:, 0::3], T.Z[:, 0:192:2], deps=z), cp(T.LC[:, 2::3], T.Z[:, 193:384:2], deps=z)]
+    lb = join(ts(T.LB[:, 1::3], T.PM[:, 0:96], OWNW, A.add, deps=qb),
+              cp(T.LB[:, 0::3], T.ZS1[:, 0::2], deps=[zs1]), cp(T.LB[:, 2::3], T.ZS1[:, 1::2], deps=[zs1]))
+
+    for k, p in enumerate(dest):
+        lists = [T.LB[:, 96 * k + 24 * n:96 * k + 24 * n + 24] for n in range(4)]
         f0, f1, f2, f3 = [T[x][:, SLW * k:SLW * k + SLW] for x in ("F0", "F1", "F2", "F3")]
-        deps = lb + [own0] + arr0
-        x0 = cp(f0, src[0], deps)
-        x1 = tt(f1, src[1], f0, A.max, deps + [x0])
-        x = join(x1, ac(f2, src[2], deps), ac(f3, src[3], deps))
-        es = feng if p in far else neng
-        send([transfer(p, [f1, f2, f3], T.W1, es, "arr1_%d" % r, 2)], x)
-        left[0] += len(es)
-    arr1 = [("sem", "arr1_%d" % q, len(feng) if q in far else len(neng)) for q in others]
+        deps = lb + own0 + arr0
+        if k == 2:
+            lc.append(cp(T.LC[:, 1::3], T.PT[:, 0:96], deps=qc))
+            join(*lc)
+        hw = SLW // 2
+        x0 = [cp(f0[:, hw * h:hw * h + hw], T.W0[:, :].indirect(lists[0][:, 12 * h:12 * h + 12]), deps) for h in range(2)]
+        x1 = [tt(f1[:, hw * h:hw * h + hw], T.W0[:, :].indirect(lists[1][:, 12 * h:12 * h + 12]), f0[:, hw * h:hw * h + hw], A.max,
+                 deps + [x0[h]]) for h in range(2)]
+        x = join(*x1, ac(f2, T.W0[:, :].indirect(lists[2]), deps), ac(f3, T.W0[:, :].indirect(lists[3]), deps))
+        send(p, [f1, f2, f3], T.W1, "arr1_%d" % r, 2, x)
 
-    pc = [T.PC0, T.PC1, T.PC2]
-    merged = [[], [], []]
-    spare = [0]
+    banks = [[T.PC0, []], [T.PC1, []], [T.PC2, []], [T.PM, lb], [T.PT, lc], [T.PK, z], [T.PV, ly], [T.PY, zy]]
+    spare, turn = [0], [0]
 
-    def pieces(win, jobs, deps, stored):
-        begin, second, end = [], [], []
-        for k, (lists, width, out) in enumerate(jobs):
-            c = spare[0]
-            spare[0] += width
-            P = pc[k][:, 0:width]
-            G2, G3, H0, H1, H2 = [T[x][:, c:c + width] for x in ("G2", "G3", "H0", "H1", "H2")]
-            src = [win[:, :].indirect(x) for x in lists]
-            g2 = [ac(G2, src[2], deps)] if k else []
-            g3 = ac(G3, src[3], deps)
-            p3 = ac(P, G3, [g3] + merged[k])
-            begin.append((H1, src[0], G2, src[1], H0, g2))
-            second.append((H2, src[1 if k else 2], H1))
-            end.append((out, H2, P, p3))
-        res, h1, h2 = [], [], []
-        for k in range(len(jobs) + 1):
-            if k < len(jobs):
-                H1, s0, G2, s1, H0, g2 = begin[k]
-                if k:
-                    h1.append(tt(H1, s0, G2, A.max, deps + g2))
-                else:
-                    h0 = cp(H0, s0, deps)
-                    h1.append(tt(H1, s1, H0, A.max, deps + [h0]))
-            if k:
-                out, H2, P, p3 = end[k - 1]
-                m = tt(out, H2, P, A.max, [h2[k - 1], p3])
-                merged[k - 1] = [m]
-                res.append(m)
-                if stored:
-                    stored(k - 1, m)
-            if k < len(jobs):
-                H2, s1, H1 = second[k]
-                h2.append(tt(H2, s1, H1, A.max, deps + [h1[k]]))
+    def pieces(win, lists, jobs, deps, out, stored):
+        js, at = [], 0
+        for nodes in jobs:
+            w, c = nodes * 24, spare[0]
+            src = [win[:, :].indirect(lists[:, 72 * n + at // 2 * 3:72 * n + (at + nodes) // 2 * 3]) for n in range(4)]
+            js.append({"w": w, "src": src, "out": out[:, at * 24:(at + nodes) * 24]})
+            js[-1].update({x: T[x][:, c:c + w] for x in ("G2", "G3", "H0", "H1", "H2")})
+            spare[0] += w
+            at += nodes
+
+        def third(j):
+            g3 = ac(j["G3"], j["src"][3], deps)
+            bank = banks[turn[0] % len(banks)]
+            turn[0] += 1
+            j["P"] = bank[0][:, 0:j["w"]]
+            if j is js[-1]:
+                j["p"] = ac(j["P"], j["G3"], [g3] + bank[1])
+            else:
+                j["p"] = mm(j["P"], T.ID[:, :], j["G3"], True, True, [g3, idm] + bank[1])
+            j["bank"] = bank
+        for k, j in enumerate(js[1:]):
+            j["g"] = ac(j["G2"], j["src"][2], deps)
+            if k == 0:
+                third(js[0])
+            third(j)
+
+        res = []
+
+        def first(j):
+            j["h"] = tt(j["H1"], j["src"][0], j["G2"], A.max, deps + [j["g"]])
+
+        def second(j):
+            j["h"] = tt(j["H2"], j["src"][2 if j is js[0] else 1], j["H1"], A.max, deps + [j["h"]])
+
+        def last(k):
+            j = js[k]
+            e = tt(j["out"], j["H2"], j["P"], A.max, [j["h"], j["p"]])
+            j["bank"][1] = [e]
+            res.append(e)
+            if stored:
+                stored(k, e)
+        h = cp(js[0]["H0"], js[0]["src"][0], deps)
+        js[0]["h"] = tt(js[0]["H1"], js[0]["src"][1], js[0]["H0"], A.max, deps + [h])
+        first(js[1])
+        second(js[0])
+        n = len(js)
+        if stored:
+            second(js[1])
+            last(0)
+            for k in range(2, n):
+                first(js[k])
+                last(k - 1)
+                second(js[k])
+        else:
+            for k in range(2, n):
+                first(js[k])
+                second(js[k - 1])
+                last(k - 2)
+            second(js[n - 1])
+            last(n - 2)
+        last(n - 1)
         return res
 
-    own1 = pieces(T.W0, [([T.LC[:, 72 * n + 24 * k:72 * n + 24 * k + 24] for n in range(4)], SLW, T.W1[:, SLW * k:SLW * k + SLW])
-                         for k in range(3)], lc + [own0] + arr0, None)
+    own1 = pieces(T.W0, T.LC, JOBS0, lc + own0 + arr0, T.W1, None)
 
-    jobs, stores, at = [], [], [0]
-    for nodes in (16, 20, 12):
-        a = at[-1]
-        c0, cw = a // 2 * 3, nodes // 2 * 3
-        jobs.append(([T.LY[:, 72 * n + c0:72 * n + c0 + cw] for n in range(4)], nodes * 24, T.YB[:, a * 24:(a + nodes) * 24]))
-        at.append(a + nodes)
+    stores = []
 
     def store(k, m):
-        a, b = at[k] * 24, at[k + 1] * 24
+        a, b = sum(JOBS1[:k]) * 24, sum(JOBS1[:k + 1]) * 24
         stores.append(ld("y", T.y[:, a:b], T.YB[:, a:b], [m]))
 
-    pieces(T.W1, jobs, ly + own1 + arr1, store)
+    pieces(T.W1, T.LY, JOBS1, ly + own1 + arr1, T.YB, store)
     op("y", None, stores, "w")
     op("g", None, [("sem", "left", left[0])], "w")
 

from concourse.bass import DstId, RemoteDMATransfer
from concourse.mybir import AluOpType, AxisListType, ActivationFunctionType

NX = 140
SCRATCH = {
    "X": ("sbuf", [128, 1152], "float32"), "TR": ("sbuf", [128, 48], "int32"), "PO": ("sbuf", [128, 4], "int32"),
    "SHN": ("sbuf", [128, 4], "int32"), "NB": ("sbuf", [128, 12], "int32"), "AC": ("sbuf", [128, 4], "int32"),
    "CT": ("sbuf", [128, 48], "int32"),
    "IP": ("sbuf", [128, 2], "int32"), "DD": ("sbuf", [128, 128], "float32"), "GI": ("sbuf", [128, 128], "float32"),
    "IM": ("sbuf", [128, 16], "int32"), "IM2": ("sbuf", [128, 16], "int32"), "MK": ("sbuf", [128, 16], "float32"),
    "C48": ("sbuf", [128, 96], "float32"), "S4": ("sbuf", [128, 4], "float32"),
    "SQ4": ("sbuf", [128, 4], "float32"), "N4": ("sbuf", [128, 4], "float32"), "NP": ("sbuf", [128, 4], "float32"),
    "NM": ("sbuf", [128, 4], "float32"), "AT": ("sbuf", [128, 112], "float32"), "I24": ("sbuf", [128, 24], "float32"),
    "B1": ("sbuf", [128, 2], "int32"), "B8": ("sbuf", [128, 2], "int32"), "BQ": ("sbuf", [128, 2], "int32"),
    "BG": ("sbuf", [128, 2], "int32"), "PG": ("sbuf", [128, 1], "float32"), "QF": ("sbuf", [128, 2], "float32"),
    "LO": ("sbuf", [128, 1], "float32"), "HI": ("sbuf", [128, 1], "float32"), "PQ": ("sbuf", [128, 2], "float32"),
    "PQ4": ("sbuf", [128, 2], "float32"),
    "SH": ("sbuf", [128, 128], "float16"), "SL": ("sbuf", [128, 128], "float16"), "ON": ("sbuf", [128, 128], "bfloat16"),
    "SHW": ("sbuf", [128, 128], "float32"), "SLW": ("sbuf", [128, 128], "float32"), "ID": ("sbuf", [128, 128], "float32"),
    "RN": ("sbuf", [128, 256], "bfloat16"), "BL": ("sbuf", [128, 32], "uint16"),
    "WT": ("sbuf", [128, 48], "float32"), "LP": ("sbuf", [128, 6], "uint16"),
    "NN": ("sbuf", [128, 96], "float32"), "LSH": ("sbuf", [128, 6], "uint16"), "SHF": ("sbuf", [128, 4], "float32"),
    "RR": ("sbuf", [128, 96], "float16"),
    "LA": ("sbuf", [128, 72], "uint16"), "OWN": ("sbuf", [128, 72], "uint16"),
    "NBU": ("sbuf", [128, 12], "uint16"), "IT": ("sbuf", [128, 16], "float32"), "IDC": ("sbuf", [128, 1], "float32"),
    "LM": ("sbuf", [128, 6], "uint16"), "CW": ("sbuf", [128, 64], "float32"), "BD": ("sbuf", [128, 512], "bfloat16"),
    "TRG": ("sbuf", [128, 96], "float32"), "MS": ("sbuf", [128, 96], "float32"),
    "OA": ("sbuf", [128, 96], "bfloat16"), "OV": ("sbuf", [128, 96], "bfloat16"), "OK": ("sbuf", [128, 96], "bfloat16"),
    "ARM": ("sbuf", [128, 192], "float32"), "Z": ("sbuf", [128, 384], "float32"), "ZY": ("sbuf", [128, 384], "float32"),
    "LS1": ("sbuf", [128, 12], "uint16"), "LS2": ("sbuf", [128, 12], "uint16"),
    "ZS1": ("sbuf", [128, 192], "float32"), "ZS2": ("sbuf", [128, 192], "float16"),
    "LB": ("sbuf", [128, 288], "uint16"), "LC": ("sbuf", [128, 288], "uint16"), "LY": ("sbuf", [128, 288], "uint16"),
    "W0": ("sbuf", [128, 2304], "float32"), "W1": ("sbuf", [128, 2304], "float32"),
    "SA": ("sbuf", [128, 1152], "float32"), "YB": ("sbuf", [128, 1152], "float32"),
    "F0": ("sbuf", [128, 1152], "float32"), "F1": ("sbuf", [128, 1152], "float32"),
    "F2": ("sbuf", [128, 1152], "float32"), "F3": ("sbuf", [128, 1152], "float32"),
    "G2": ("sbuf", [128, 2304], "float32"), "G3": ("sbuf", [128, 2304], "float32"),
    "H0": ("sbuf", [128, 2304], "float32"), "H1": ("sbuf", [128, 2304], "float32"), "H2": ("sbuf", [128, 2304], "float32"),
    "PT": ("psum", [128, 512], "float32"), "PY": ("psum", [128, 512], "float32"), "PV": ("psum", [128, 512], "float32"),
    "PK": ("psum", [128, 512], "float32"), "PM": ("psum", [128, 512], "float32"),
    "PC0": ("psum", [128, 512], "float32"), "PC1": ("psum", [128, 512], "float32"), "PC2": ("psum", [128, 512], "float32"),
}
SEMAPHORES = ["left"] + ["arr%d_%d" % (t, q) for t in range(2) for q in range(4)] + ["x%d" % k for k in range(NX)]
OWNW, SLW = 48 * 24, 16 * 24
JOBS0 = [8, 12, 12, 16]
JOBS1 = [8, 12, 16, 12]


def place(q, p):
    return OWNW + SLW * (q if q < p else q - 1)


def rank_program(g, core, T, topo):
    r = T.rank_of(core)
    if r is None:
        return
    A, ACT = AluOpType, ActivationFunctionType
    ops = []

    def op(q, f, deps=(), kind="c"):
        ops.append({"q": q, "f": f, "deps": list(deps), "kind": kind, "grp": len(ops)})
        return len(ops) - 1

    def join(*ks):
        for k in ks:
            ops[k]["grp"] = ks[0]
        return list(ks)

    v, s, t = g.vector, g.scalar, g.tensor
    queues = {"v": v, "s": s, "t": t, "g": g, "y": g.sync}

    def ts(out, in0, s1, op0, s2=None, op1=None, deps=()):
        if op1 is None:
            return op("v", lambda: v.tensor_scalar(out, in0, s1, None, op0), deps)
        return op("v", lambda: v.tensor_scalar(out, in0, s1, s2, op0, op1), deps)

    def tt(out, a, b, o, deps=()):
        return op("v", lambda: v.tensor_tensor(out, a, b, o), deps)

    def cp(out, a, deps=()):
        return op("v", lambda: v.tensor_copy(out, a), deps)

    def ac(out, a, deps=()):
        return op("s", lambda: s.activation(out, a, ACT.Copy), deps)

    def mm(out, lhs, rhs, start, stop, deps):
        return op("t", lambda: t.matmul(out, lhs, rhs, start, stop), deps)

    def ld(q, out, in_, deps=()):
        return op(q, lambda: queues[q].dma_start(out, in_), deps, "d")

    others = [p for p in range(len(T.cores)) if p != r]
    near = [p for p in others if T.cores[p] in topo.cores_of(core)]
    far = [p for p in others if p not in near]
    far.sort(key=lambda p: topo.die(T.cores[p]) != topo.die(core))
    dest = far + near
    feng = topo.engines(core, T.cores[far[0]])
    neng = [e for e in topo.engines(core, T.cores[near[0]]) if e not in feng]

    def bits(es):
        return sum(1 << e for e in es)

    d_ra = ld("y", T.TR[:, 0:24], T.rel[:, 0:384])
    d_po = ld("s", T.PO[:, 0:3], T.pose[:, :])
    d_rd = ld("y", T.TR[:, 24:48], T.rel[:, 192:576])
    d_sh = ld("s", T.SHN[:, 0:4], T.shown[:, :])
    d_x = ld("s", T.X[:, :], T.x[:, :])
    d_ac = ld("s", T.AC[:, 0:3], T.act[:, :])
    d_nb = ld("s", T.NB[:, 0:12], T.nbr[:, :])
    d_ct = join(ld("s", T.CT[:, 0:24], T.ct[:, 0:384]), ld("s", T.CT[:, 24:48], T.ct[:, 192:576]))
    join(d_ra, d_rd)

    def iota(out, pat, base, cm, f32=True):
        if f32:
            return op("g", lambda: g.iota(out, pat, base, cm, allow_small_or_imprecise_dtypes=True))
        return op("g", lambda: g.iota(out, pat, base, cm))

    i_p = iota(T.IP[:, :], [[0, 2]], 0, 1, False)
    i_d = iota(T.DD[:, :], [[1, 128]], 0, -1)
    i_c = iota(T.C48[:, :], [[0, 2], [24, 48]], 0, 0)
    i_m = iota(T.IM[:, :], [[1, 16]], 0, -1, False)
    i_g = iota(T.GI[:, :], [[1, 8], [0, 16]], 0, 0)
    i_4 = iota(T.S4[:, :], [[24, 2], [8, 2]], -48, 0)
    i_24 = iota(T.I24[:, :], [[1, 24]], 0, 0)
    i_n = iota(T.N4[:, :], [[48, 4]], 0, 0)
    hole = 48 + 16 * r + 16
    i_a = [iota(T.AT[:, 0:hole], [[24, hole]], 0, 0)]
    if hole < 112:
        i_a.append(iota(T.AT[:, hole:112], [[24, 112 - hole]], 24 * (hole - 16), 0))
    join(*i_a)

    c_b = join(ts(T.B1[:, :], T.IP[:, :], 1, A.bitwise_and, deps=[i_p]),
               ts(T.B8[:, :], T.IP[:, :], 8, A.bitwise_and, deps=[i_p]),
               ts(T.BQ[:, :], T.IP[:, :], 15, A.bitwise_and, deps=[i_p]),
               ts(T.BG[:, :], T.IP[:, :], 4, A.arith_shift_right, deps=[i_p]))
    c_m = join(ts(T.LO[:, :], T.B8[:, 0:1], 0, A.is_equal, deps=c_b),
               ts(T.HI[:, :], T.B8[:, 0:1], 0, A.is_gt, deps=c_b),
               ts(T.PQ[:, 0:1], T.B1[:, 0:1], 48, A.mult, deps=c_b),
               ts(T.PQ[:, 1:2], T.B1[:, 0:1], -48, A.mult, 48, A.add, deps=c_b),
               cp(T.PG[:, :], T.BG[:, 0:1], deps=c_b),
               cp(T.QF[:, 0:1], T.BQ[:, 0:1], deps=c_b))
    c_s = join(ts(T.SH[:, :], T.DD[:, :], -8, A.is_equal, T.HI[:, :], A.mult, deps=[i_d] + c_m),
               ts(T.SL[:, :], T.DD[:, :], 8, A.is_equal, T.LO[:, :], A.mult, deps=[i_d] + c_m))
    c_f = join(ts(T.SHW[:, :], T.DD[:, :], -8, A.is_equal, T.HI[:, :], A.mult, deps=[i_d] + c_m),
               ts(T.SLW[:, :], T.DD[:, :], 8, A.is_equal, T.LO[:, :], A.mult, deps=[i_d] + c_m))
    im2 = ts(T.IM2[:, :], T.IM[:, :], 15, A.bitwise_and, deps=[i_m])
    zc = op("v", lambda: v.memset(T.CW[:, 48:64], 0.0))
    mk = ts(T.MK[:, :], T.IM2[:, :], 0, A.is_equal, deps=[im2])
    c_q = ts(T.QF[:, 1:2], T.QF[:, 0:1], 8, A.add, T.HI[:, :], A.mult, deps=c_m)
    on = ts(T.ON[:, :], T.GI[:, :], T.PG[:, :], A.is_equal, deps=[i_g] + c_m)
    sq4 = ts(T.SQ4[:, :], T.S4[:, :], T.QF[:, 0:1], A.add, deps=[i_4] + c_m)

    lp = join(*[ts(T.LP[:, 3 * k:3 * k + 3], T.PO[:, 0:3], 24 * k, A.add, deps=[d_po]) for k in range(2)])
    nn = tt(T.NN[:, :], T.TR[:, :].indirect(T.LP[:, 0:6]), T.C48[:, :], A.add, deps=lp + [d_ra, d_rd, i_c])
    shf = cp(T.SHF[:, :], T.SHN[:, :], deps=[d_sh])
    wt = cp(T.WT[:, :], T.TR[:, :], deps=[d_ra, d_rd])
    lsh = join(*[ts(T.LSH[:, k::3], T.PQ[:, :], T.SHF[:, p:p + 1], A.add, deps=c_m + [shf]) for k, p in enumerate(dest)])
    rr = cp(T.RR[:, :], T.NN[:, :].indirect(T.LSH[:, 0:6]), deps=[nn] + lsh)
    trg = ac(T.TRG[:, :], T.WT[:, :].indirect(T.LP[:, 0:6]), deps=lp + [wt])
    idt = tt(T.IT[:, :], T.WT[:, 0:16], T.MK[:, :], A.mult, deps=[wt, mk])
    la = [cp(T.LA[:, 0::3], T.RR[:, 0:48:2], deps=[rr]), cp(T.LA[:, 2::3], T.RR[:, 1:48:2], deps=[rr])]
    qa = join(mm(T.PT[:, 0:24], T.SH[:, :], T.RR[:, 48:96:2], True, False, [rr] + c_s),
              mm(T.PT[:, 0:24], T.SL[:, :], T.RR[:, 49:96:2], False, True, [rr] + c_s))
    idc = op("v", lambda: v.tensor_reduce(T.IDC[:, :], T.IT[:, :], AxisListType.X, A.add), [idt])
    qo = join(mm(T.PM[:, 0:24], T.SHW[:, :], T.NN[:, 48:96:2], True, False, [nn] + c_f),
              mm(T.PM[:, 0:24], T.SLW[:, :], T.NN[:, 1:48:2], False, True, [nn] + c_f))
    ow = [cp(T.OWN[:, 0::3], T.NN[:, 0:48:2], deps=[nn])]
    la.append(cp(T.LA[:, 1::3], T.PT[:, 0:24], deps=qa))
    join(*la)

    bl = join(*[ts(T.BL[:, 8 * k:8 * k + 8], T.ON[:, 0::16], T.SQ4[:, k:k + 1], A.mult, 48, A.add, deps=[on, sq4]) for k in range(4)])
    ow.append(cp(T.OWN[:, 2::3], T.NN[:, 49:96:2], deps=[nn]))
    ow.append(cp(T.OWN[:, 1::3], T.PM[:, 0:24], deps=qo))
    join(*ow)

    def transfer(p, srcs, win, es, arr, alu=0):
        rid, pid = topo.addr(T.cores[p], core)
        c = place(r, p)
        return RemoteDMATransfer(srcs=srcs, dsts=[win[:, c:c + SLW]], dst_ids=[DstId(rid=rid, pnc=pid)],
                                 dma_engine_mask=bits(es), remote_sem=T.sem[arr], alu_op=alu)

    left = [0]

    def send(p, srcs, win, arr, alu, deps):
        es = feng if p in far else neng
        left[0] += len(es)
        x = transfer(p, srcs, win, es, arr, alu)
        return op("g", lambda: g.remote_dma_fused([x], local_sem=T.sem["left"]), deps, "r")

    for k, p in enumerate(dest):
        a, b = SLW * k, SLW * k + SLW // 2
        x = join(cp(T.SA[:, a:b], T.X[:, :].indirect(T.LA[:, 24 * k:24 * k + 12]), deps=la + [d_x]),
                 ac(T.SA[:, b:a + SLW], T.X[:, :].indirect(T.LA[:, 24 * k + 12:24 * k + 24]), deps=la + [d_x]))
        send(p, [T.SA[:, a:a + SLW]], T.W0, "arr0_%d" % r, 0, x)
    arr0, arr1 = [[("sem", "arr%d_%d" % (k, q), len(feng) if q in far else len(neng)) for q in others] for k in range(2)]

    lm = join(*[cp(T.LM[:, 3 * k:3 * k + 3], T.AC[:, 0:3], deps=[d_ac]) for k in range(2)])
    cw = join(cp(T.CW[:, 0:24], T.CT[:, 0:24], deps=d_ct), ts(T.CW[:, 24:48], T.CT[:, 24:48], T.HI[:, :], A.mult, deps=d_ct + c_m))
    ms = ac(T.MS[:, :], T.I24[:, :].indirect(T.LM[:, :]), deps=lm + [i_24])
    nbu = cp(T.NBU[:, :], T.NB[:, :], deps=[d_nb])
    bd = join(ac(T.BD[:, 0:256], T.CW[:, :].indirect(T.BL[:, 0:16]), deps=bl + cw + [zc]),
              cp(T.BD[:, 256:512], T.CW[:, :].indirect(T.BL[:, 16:32]), deps=bl + cw + [zc]))
    oa = tt(T.OA[:, :], T.TRG[:, :], T.MS[:, :], A.is_equal, deps=[trg, ms])
    arm = ac(T.ARM[:, :], T.AT[:, :].indirect(T.NBU[:, :]), deps=i_a + [nbu])

    def rows(out, oh, deps):
        return join(*[mm(out[:, 48 * h:48 * h + 48], T.BD[:, 256 * k + 128 * h:256 * k + 128 * h + 128], oh[:, 48 * k:48 * k + 48],
                         k == 0, k == 1, deps) for h in range(2) for k in range(2)])

    def plus(out, P, deps):
        return join(*[tt(out[:, 192 * h + 48 * n:192 * h + 48 * n + 48], T.ARM[:, 48 * n:48 * n + 48], P[:, 48 * h:48 * h + 48], A.add, deps)
                      for h in range(2) for n in range(4)])

    def middle(P, up, down, even, odd, deps):
        return join(mm(P, up, even, True, False, deps), mm(P, down, odd, False, True, deps))

    qy = rows(T.PY, T.OA, [oa] + bd)
    c_r = join(ts(T.RN[:, 0:128], T.ON[:, :], T.QF[:, 0:1], A.mult, deps=[on] + c_m),
               ts(T.RN[:, 128:256], T.ON[:, :], T.QF[:, 1:2], A.mult, deps=[on, c_q]))
    c_p = ts(T.PQ4[:, :], T.PQ[:, :], 4, A.mult, deps=c_m)
    idm = ts(T.ID[:, :], T.DD[:, :], 0, A.is_equal, deps=[i_d])
    c_np = join(ts(T.NP[:, :], T.N4[:, :], T.PQ4[:, 0:1], A.add, deps=[i_n, c_p]),
                ts(T.NM[:, :], T.N4[:, :], T.PQ4[:, 1:2], A.add, deps=[i_n, c_p]))
    own0 = [ac(T.W0[:, 0:OWNW], T.X[:, :].indirect(T.OWN[:, :]), deps=ow + [d_x])]
    ov = ts(T.OV[:, :], T.PY[:, 0:96], T.IDC[:, :], A.is_equal, deps=qy + [idc])
    qv = join(*[mm(T.PV[:, 48 * h:48 * h + 48], T.RN[:, 128 * k:128 * k + 128], T.OV[:, 48 * k:48 * k + 48], k == 0, k == 1, [ov] + c_r)
                for h in range(2) for k in range(2)])
    zy = plus(T.ZY, T.PY, qy + [arm])
    ok = tt(T.OK[:, :], T.TRG[:, :], T.PV[:, 0:96], A.is_equal, deps=qv + [trg])
    qk = rows(T.PK, T.OK, [ok] + bd)
    ls = join(*([ts(T.LS2[:, 4 * k:4 * k + 4], T.NM[:, :], T.SHF[:, p:p + 1], A.add, deps=c_np + [shf]) for k, p in enumerate(dest)] +
                [ts(T.LS1[:, 4 * k:4 * k + 4], T.NP[:, :], T.SHF[:, p:p + 1], A.add, deps=c_np + [shf]) for k, p in enumerate(dest)]))
    qz = middle(T.PV[:, 0:96], T.SHW[:, :], T.SLW[:, :], T.ZY[:, 192:384:2], T.ZY[:, 1:192:2], zy + c_f + [ok])
    ly = [cp(T.LY[:, 0::3], T.ZY[:, 0:192:2], deps=zy)]
    z = plus(T.Z, T.PK, qk + [arm])
    ly.append(cp(T.LY[:, 2::3], T.ZY[:, 193:384:2], deps=zy))
    zs2 = ts(T.ZS2[:, :], T.Z[:, :].indirect(T.LS2[:, :]), -OWNW, A.add, deps=z + ls)
    zs1 = ac(T.ZS1[:, :], T.Z[:, :].indirect(T.LS1[:, :]), deps=z + ls)
    qb = middle(T.PM[:, 0:96], T.SH[:, :], T.SL[:, :], T.ZS2[:, 0::2], T.ZS2[:, 1::2], [zs2] + c_s + ow)
    qc = middle(T.PT[:, 0:96], T.SHW[:, :], T.SLW[:, :], T.Z[:, 192:384:2], T.Z[:, 1:192:2], z + c_f + la)
    ly.append(cp(T.LY[:, 1::3], T.PV[:, 0:96], deps=qz))
    join(*ly)
    lc = [cp(T.LC[:, 0::3], T.Z[:, 0:192:2], deps=z), cp(T.LC[:, 2::3], T.Z[:, 193:384:2], deps=z)]
    lb = join(ts(T.LB[:, 1::3], T.PM[:, 0:96], OWNW, A.add, deps=qb),
              cp(T.LB[:, 0::3], T.ZS1[:, 0::2], deps=[zs1]), cp(T.LB[:, 2::3], T.ZS1[:, 1::2], deps=[zs1]))

    for k, p in enumerate(dest):
        lists = [T.LB[:, 96 * k + 24 * n:96 * k + 24 * n + 24] for n in range(4)]
        f0, f1, f2, f3 = [T[x][:, SLW * k:SLW * k + SLW] for x in ("F0", "F1", "F2", "F3")]
        deps = lb + own0 + arr0
        if k == 2:
            lc.append(cp(T.LC[:, 1::3], T.PT[:, 0:96], deps=qc))
            join(*lc)
        hw = SLW // 2
        x0 = [cp(f0[:, hw * h:hw * h + hw], T.W0[:, :].indirect(lists[0][:, 12 * h:12 * h + 12]), deps) for h in range(2)]
        x1 = [tt(f1[:, hw * h:hw * h + hw], T.W0[:, :].indirect(lists[1][:, 12 * h:12 * h + 12]), f0[:, hw * h:hw * h + hw], A.max,
                 deps + [x0[h]]) for h in range(2)]
        x = join(*x1, ac(f2, T.W0[:, :].indirect(lists[2]), deps), ac(f3, T.W0[:, :].indirect(lists[3]), deps))
        send(p, [f1, f2, f3], T.W1, "arr1_%d" % r, 2, x)

    banks = [[T.PC0, []], [T.PC1, []], [T.PC2, []], [T.PM, lb], [T.PT, lc], [T.PK, z], [T.PV, ly], [T.PY, zy]]
    spare, turn = [0], [0]

    def pieces(win, lists, jobs, deps, out, stored):
        js, at = [], 0
        for nodes in jobs:
            w, c = nodes * 24, spare[0]
            src = [win[:, :].indirect(lists[:, 72 * n + at // 2 * 3:72 * n + (at + nodes) // 2 * 3]) for n in range(4)]
            js.append({"w": w, "src": src, "out": out[:, at * 24:(at + nodes) * 24]})
            js[-1].update({x: T[x][:, c:c + w] for x in ("G2", "G3", "H0", "H1", "H2")})
            spare[0] += w
            at += nodes

        def third(j):
            g3 = ac(j["G3"], j["src"][3], deps)
            bank = banks[turn[0] % len(banks)]
            turn[0] += 1
            j["P"] = bank[0][:, 0:j["w"]]
            if j is js[-1]:
                j["p"] = ac(j["P"], j["G3"], [g3] + bank[1])
            else:
                j["p"] = mm(j["P"], T.ID[:, :], j["G3"], True, True, [g3, idm] + bank[1])
            j["bank"] = bank
        for k, j in enumerate(js[1:]):
            j["g"] = ac(j["G2"], j["src"][2], deps)
            if k == 0:
                third(js[0])
            third(j)

        res = []

        def first(j):
            j["h"] = tt(j["H1"], j["src"][0], j["G2"], A.max, deps + [j["g"]])

        def second(j):
            j["h"] = tt(j["H2"], j["src"][2 if j is js[0] else 1], j["H1"], A.max, deps + [j["h"]])

        def last(k):
            j = js[k]
            e = tt(j["out"], j["H2"], j["P"], A.max, [j["h"], j["p"]])
            j["bank"][1] = [e]
            res.append(e)
            if stored:
                stored(k, e)
        h = cp(js[0]["H0"], js[0]["src"][0], deps)
        js[0]["h"] = tt(js[0]["H1"], js[0]["src"][1], js[0]["H0"], A.max, deps + [h])
        first(js[1])
        second(js[0])
        n = len(js)
        if stored:
            second(js[1])
            last(0)
            for k in range(2, n):
                first(js[k])
                last(k - 1)
                second(js[k])
        else:
            for k in range(2, n):
                first(js[k])
                second(js[k - 1])
                last(k - 2)
            second(js[n - 1])
            last(n - 2)
        last(n - 1)
        return res

    own1 = pieces(T.W0, T.LC, JOBS0, lc + own0 + arr0, T.W1, None)

    stores = []

    def store(k, m):
        a, b = sum(JOBS1[:k]) * 24, sum(JOBS1[:k + 1]) * 24
        stores.append(ld("y", T.y[:, a:b], T.YB[:, a:b], [m]))

    pieces(T.W1, T.LY, JOBS1, ly + own1 + arr1, T.YB, store)
    op("y", None, stores, "w")
    op("g", None, [("sem", "left", left[0])], "w")

    used, total = set(), {}
    for o in ops:
        used.update(ops[d]["grp"] for d in o["deps"] if not isinstance(d, tuple))
    for o in ops:
        total[o["grp"]] = total.get(o["grp"], 0) + (16 if o["kind"] == "d" else 1)
    names = {k: "x%d" % n for n, k in enumerate(sorted(used))}
    done = {q: {} for q in queues}

    def wait(q, name, val):
        if done[q].get(name, 0) < val:
            queues[q].wait_ge(T.sem[name], val)
            done[q][name] = val

    for o in ops:
        for d in o["deps"]:
            if isinstance(d, tuple):
                wait(o["q"], d[1], d[2])
            else:
                k = ops[d]["grp"]
                wait(o["q"], names[k], total[k])
        if o["kind"] != "w":
            ins = o["f"]()
            if o["grp"] in names:
                ins.then_inc(T.sem[names[o["grp"]]], 16 if o["kind"] == "d" else 1)
